import numpy as np
import ml_dtypes


def mxq(x, axis, fmt="e4m3"):
    dtype, down = {"e4m3": (ml_dtypes.float8_e4m3fn, 7), "e5m2": (ml_dtypes.float8_e5m2, 14)}[fmt]
    v = np.moveaxis(np.asarray(x, np.float32).astype(ml_dtypes.bfloat16).astype(np.float64), axis, -1)
    blocks = v.reshape(v.shape[:-1] + (-1, 32))
    amax = np.abs(blocks).max(-1, keepdims=True)
    byte = np.maximum(np.where(amax > 0, np.frexp(amax)[1] - 1 + 127, 0) - down, 1)
    scale = np.exp2(byte - 127.0)
    codes = (blocks / scale).astype(np.float32).astype(dtype).astype(np.float64)
    return np.moveaxis((codes * scale).reshape(v.shape), -1, axis)


WIDE = False


def mx_kscale(k):
    if not WIDE:
        return np.ones(k)
    levels = np.array([10, -10, 5, -5, 0])
    if k % 512:
        return np.exp2(np.random.permutation(np.resize(levels, k // 32))).repeat(32)
    a = np.empty((k // 512, 16))
    for p in range(k // 512):
        a[p, :8] = np.random.permutation(np.resize(levels, 8))
        for g in range(8):
            far = levels[np.abs(levels - a[p, g]) >= 10]
            a[p, g + 8] = far[np.random.randint(len(far))]
    return np.exp2(a.ravel()).repeat(32)


BF16 = ml_dtypes.bfloat16


def bf(x):
    return np.asarray(x, np.float32).astype(BF16)


def f64(x):
    return np.asarray(x).astype(np.float64)


E2M1 = np.array([0.0, 0.5, 1.0, 1.5, 2.0, 3.0, 4.0, 6.0, -0.0, -0.5, -1.0, -1.5, -2.0, -3.0, -4.0, -6.0])


def pack_weight(w, fmt):
    k, n = w.shape
    w = f64(bf(w)).reshape(k // 32, 32, n)
    amax = np.abs(w).max(1)
    if fmt == "e4m3":
        byte = np.frexp(amax)[1] - 1 + 127 - 7
    else:
        mant, ex = np.frexp(amax / 6.0)
        byte = np.where(mant > 0.5, ex, ex - 1) + 127
    byte = np.clip(np.where(amax > 0, byte, 1), 1, 254)
    scaled = (w * np.exp2(127.0 - byte)[:, None, :]).reshape(k, n).astype(np.float32)
    by_word = np.ascontiguousarray(scaled.reshape(k // 512, 128, 4, n).transpose(0, 1, 3, 2))
    if fmt == "e4m3":
        words = by_word.astype(ml_dtypes.float8_e4m3fn).view(np.uint8)
    else:
        c = by_word.astype(ml_dtypes.float4_e2m1fn).view(np.uint8) & 0xF
        words = c[..., 0::2] | (c[..., 1::2] << 4)
    return np.ascontiguousarray(words), np.ascontiguousarray(byte.astype(np.uint8).reshape(k // 512, 16, n))


def unpack_weight(words, scales, fmt):
    g, p, n, _ = words.shape
    if fmt == "e4m3":
        vals = np.ascontiguousarray(words).view(ml_dtypes.float8_e4m3fn).astype(np.float64)
    else:
        nib = np.empty((g, p, n, 4), np.uint8)
        nib[..., 0::2] = words & 0xF
        nib[..., 1::2] = words >> 4
        vals = E2M1[nib]
    vals = vals * np.repeat(np.exp2(scales.astype(np.float64) - 127.0), 8, axis=1)[..., None]
    return vals.transpose(0, 1, 3, 2).reshape(g * 512, n)
def pack4(w):
    words, scales = pack_weight(w, "e2m1")
    return words.reshape(words.shape[0], 128, -1), scales


def unpack4(words, scales):
    return unpack_weight(words.reshape(words.shape[0], 128, -1, 2), scales, "e2m1")


def planes(Y):
    n, m = Y.shape
    b = f64(bf(Y)).reshape(n // 32, 32, m)
    amax = np.abs(b).max(1)
    byte = np.clip(np.where(amax > 0, np.frexp(amax)[1] - 1 + 127 - 7, 1), 1, 254)
    codes = (b * np.exp2(127.0 - byte)[:, None, :]).reshape(n, m).astype(np.float32).astype(ml_dtypes.float8_e4m3fn).view(np.uint8)
    words = codes.reshape(n // 512, 128, 4, m).transpose(0, 1, 3, 2)
    return np.ascontiguousarray(words), np.ascontiguousarray(byte.astype(np.uint8).reshape(n // 512, 16, m))


G, N, D, C = 8, 256, 1024, 512
ETA = 0.125


def stable_softplus(t):
    return np.maximum(t, 0.0) + np.log1p(np.exp(-np.abs(t)))


def sigmoid(t):
    return 1.0 / (1.0 + np.exp(-t))


def group_losses(z, y, a, b):
    n = z.shape[1]
    loss = np.sum(stable_softplus(z) - y * z, axis=-1)
    return np.sum(a * b * loss, axis=1) / n


def setup_inputs():
    s = mx_kscale(D)
    u = mx_kscale(G * N).reshape(G, N)
    h = np.random.standard_normal((G, N, D)) + 0.5 * np.random.standard_normal((G, 1, D))
    w = np.random.standard_normal((D, C)) / np.sqrt(D)
    y = np.random.uniform(0.0, 1.0, (G, N, C))
    a = 0.5 * (1.0 + 0.2 * np.random.standard_normal((G, N)) + 16.0 / C * np.random.standard_normal((G, 1)))
    b = 0.5 * (1.0 + 0.2 * np.random.standard_normal((G, N)) + 16.0 / C * np.random.standard_normal((G, 1)))
    adj = 4.0 * np.random.standard_normal(G)
    c = 4.0 * (1.0 + 0.1 * np.random.standard_normal(D))
    words, scales = pack4(w / s[:, None])
    return {"h": bf(h * s), "w_words": words, "w_scales": scales, "y": bf(y), "a": bf(a * u), "b": bf(b / u), "adj": bf(adj), "c": bf(c / s)}


def core(h, w_words, w_scales, y, a, b, adj, c):
    h, y, a, b, adj, c = f64(h), f64(y), f64(a), f64(b), f64(adj), f64(c)
    n = h.shape[1]
    z = mxq(h, 2, "e4m3") @ unpack4(w_words, w_scales)
    group_loss = group_losses(z, y, a, b)
    v = ETA * (group_loss + adj)
    e = np.exp(v - v.max(axis=0, keepdims=True))
    q = e / e.sum(axis=0, keepdims=True)
    weighted_h = a[:, :, None] * h
    row_weight = b * q[:, None]
    delta = row_weight[:, :, None] * (sigmoid(z) - y)
    wh = mxq(weighted_h.reshape(G * N, D), 0, "e4m3")
    dl = mxq(delta.reshape(G * N, C), 0, "e4m3")
    grad = (wh.T @ dl) / n
    return 32.0 * c[:, None] * grad


def reference(h, w_words, w_scales, y, a, b, adj, c):
    R_out = core(h, w_words, w_scales, y, a, b, adj, c)
    words, scales = planes(R_out)
    return R_out, words, scales

@@ -1,0 +1,434 @@
+from contextlib import ExitStack
+
+import concourse.mybir as mybir
+from concourse.masks import make_identity
+
+F32 = mybir.dt.float32
+BF16 = mybir.dt.bfloat16
+U32 = mybir.dt.uint32
+I32 = mybir.dt.int32
+U8 = mybir.dt.uint8
+FP8X4 = mybir.dt.float8_e4m3fn_x4
+FP4X4 = mybir.dt.float4_e2m1fn_x4
+ACT = mybir.ActivationFunctionType
+ALU = mybir.AluOpType
+AX = mybir.AxisListType
+
+N_GROUPS, N_EX, D, C = 8, 256, 1024, 512
+TOKENS = N_GROUPS * N_EX
+P = 128
+PASSES = TOKENS // 512
+TILES = TOKENS // P
+FLOPS = 2 * (2 * TOKENS * D * C)
+KH = 256
+V_COLS = 128
+V_PIECES = {(0, 1, 0): 0, (0, 1, 1): 1, (0, 0, 1): 1}
+WQ_STEPS = {3: 0, 5: 1, 7: 2}
+
+
+def tile_groupdrologsumexppreconditionedgradient_x2_kernel(
+    tc, h, w_words, w_scales, y, a, b, adj, c, out_0, out_1, out_2
+):
+    nc = tc.nc
+    with ExitStack() as ctx:
+        keep = ctx.enter_context(tc.tile_pool(name="keep", bufs=1))
+        work = ctx.enter_context(tc.tile_pool(name="work", bufs=3))
+        psum = ctx.enter_context(tc.psum_pool(name="psum", bufs=1))
+        ctx.enter_context(tc.manual_schedule())
+
+        def bank(index, shape, what):
+            return psum.tile(shape, F32, name="%s_b%d" % (what, index), tag="bank%d" % index, bufs=1)
+
+        x = [keep.tile([P, 4, D], BF16, name="x%d" % g) for g in range(PASSES)]
+        yt = [keep.tile([P, 4, C], BF16, name="y%d" % g) for g in range(PASSES)]
+        bd = [keep.tile([P, 4, C], F32, name="bd%d" % g) for g in range(PASSES)]
+        w_codes = [keep.tile([P, D], U32, name="wc%d" % g, align_bytes=64) for g in range(PASSES)]
+        w_planes = [keep.tile([P, D], U8, name="wp%d" % g, align_bytes=64) for g in range(PASSES)]
+        d_codes = [keep.tile([P, C], U32, name="dc%d" % g, align_bytes=64) for g in range(PASSES)]
+        d_planes = [keep.tile([P, C], U8, name="dp%d" % g, align_bytes=64) for g in range(PASSES)]
+        ww = keep.tile([P, 2, 2 * C], U8, name="ww", align_bytes=64)
+        ws = keep.tile([P, 2, C], U8, name="ws", align_bytes=64)
+        a_bf = keep.tile([P, PASSES, 4], BF16, name="a_bf")
+        b_bf = keep.tile([P, PASSES, 4], BF16, name="b_bf")
+        c_bf = keep.tile([P, 2, 4], BF16, name="c_bf")
+        adj_bf = keep.tile([1, N_GROUPS], BF16, name="adj_bf")
+        c8 = keep.tile([P, 2, 4], F32, name="c8")
+        wab = keep.tile([P, TILES], F32, name="wab")
+        wm = keep.tile([P, 2, TILES], F32, name="wm")
+        ones = keep.tile([P, P], F32, name="ones")
+        ident_f = keep.tile([P, P], F32, name="ident_f")
+        ident_b = keep.tile([P, P], BF16, name="ident_b")
+        dg = keep.tile([P, TILES, P], BF16, name="dg")
+        abs_acc = keep.tile([P, TILES], F32, name="abs_acc")
+        yz_acc = keep.tile([P, TILES], F32, name="yz_acc")
+        prods = keep.tile([P, TILES, 8], F32, name="prods")
+
+        h_rows = h.rearrange("g n d -> (g n) d").rearrange("(q p j) d -> q p j d", p=P, j=4)
+        y_rows = y.rearrange("g n k -> (g n) k").rearrange("(q p j) k -> q p j k", p=P, j=4)
+        nc.vector.memset(ws[:].rearrange("p g n -> p (g n)").bitcast(I32), 0)
+        make_identity(nc, ident_f[:])
+        nc.gpsimd.dma_start(out=b_bf[:], in_=b.rearrange("g n -> (g n)").rearrange("(q p j) -> p q j", p=P, j=4))
+        nc.gpsimd.dma_start(out=a_bf[:], in_=a.rearrange("g n -> (g n)").rearrange("(q p j) -> p q j", p=P, j=4))
+        nc.sync.dma_start(out=x[0][:, 0, :], in_=h_rows[0][:, 0, :])
+        for q in range(4):
+            nc.scalar.dma_start(
+                out=ws[32 * q : 32 * q + 4, :, :].bitcast(I32),
+                in_=w_scales[:, 4 * q : 4 * q + 4, :].rearrange("g r n -> r g n").bitcast(I32),
+            )
+        nc.sync.dma_start(out=ww[:].bitcast(I32), in_=w_words.rearrange("g p n -> p g n").bitcast(I32))
+        for j in range(1, 4):
+            nc.sync.dma_start(out=x[0][:, j, :], in_=h_rows[0][:, j, :])
+        nc.sync.dma_start(out=yt[0][:], in_=y_rows[0])
+        nc.gpsimd.dma_start(out=adj_bf[:], in_=adj.rearrange("(o g) -> o g", o=1))
+        nc.gpsimd.dma_start(out=c_bf[:], in_=c.rearrange("(g p t) -> p g t", p=P, t=4))
+        for q in range(1, PASSES):
+            nc.sync.dma_start(out=x[q][:, 0:2, :], in_=h_rows[q][:, 0:2, :])
+            nc.sync.dma_start(out=x[q][:, 2:4, :], in_=h_rows[q][:, 2:4, :])
+            nc.sync.dma_start(out=yt[q][:], in_=y_rows[q])
+
+        a_col = a_bf[:].rearrange("p q j -> p (q j)")
+        b_col = b_bf[:].rearrange("p q j -> p (q j)")
+        nc.vector.tensor_copy(out=ident_b[:], in_=ident_f[:])
+        nc.vector.memset(ones[:], 1.0)
+        warm = keep.tile([P, 1], F32, name="warm")
+        nc.scalar.activation(out=warm[:], in_=ones[:, 0:1], func=ACT.Sigmoid)
+        nc.vector.memset(wm[:], 0.0)
+
+        def diag_b(i):
+            nc.vector.tensor_scalar(
+                out=dg[:, i, :], in0=ident_b[:], scalar1=b_col[:, i : i + 1], scalar2=None, op0=ALU.mult
+            )
+
+        def weights():
+            nc.vector.scalar_tensor_tensor(
+                out=wab[:], in0=a_col, scalar=1.0 / 2048, in1=b_col, op0=ALU.mult, op1=ALU.mult
+            )
+            nc.vector.tensor_scalar(
+                out=c8[:].rearrange("p g t -> p (g t)"), in0=c_bf[:].rearrange("p g t -> p (g t)"),
+                scalar1=0.125, scalar2=None, op0=ALU.mult,
+            )
+            for half in range(2):
+                rows = slice(64 * half, 64 * half + 64)
+                nc.vector.tensor_copy(out=wm[rows, half, :], in_=wab[rows, :])
+
+
+        tiles = {}
+
+        def tr(i):
+            q, j = divmod(i, 4)
+            words = x[q][:, j, :].bitcast(F32)
+            t = bank(i % 2, [P, 2, 2, P], "tr")
+            for g in range(2):
+                for u in range(2):
+                    nc.tensor.transpose(t[:, g, u, :], words[:, 256 * g + u : 256 * (g + 1) : 2], ident_f[:])
+            tiles["tr", i] = t
+
+        def copy(i):
+            kk, half = divmod(i, 2)
+            if half == 0:
+                tiles["hq", kk] = work.tile([P, 2, D], BF16, name="hq", tag="hq", bufs=2, align_bytes=64)
+            nc.scalar.copy(
+                out=tiles["hq", kk][:, half, :].bitcast(F32).rearrange("p (g r u) -> p g r u", g=2, u=2),
+                in_=tiles["tr", i][:].rearrange("p g u r -> p g r u"),
+            )
+
+        def quant(kk):
+            hc = work.tile([P, 2, 256], U32, name="hc", tag="hc", bufs=2, align_bytes=64)
+            hs = work.tile([P, 2, 256], U8, name="hs", tag="hs", bufs=2, align_bytes=64)
+            nc.vector.quantize_mx(
+                out=hc[:].rearrange("p i w -> p (i w)").bitcast(FP8X4), scales=hs[:].rearrange("p i w -> p (i w)"),
+                in_=tiles["hq", kk][:].rearrange("p i d -> p (i d)"),
+            )
+            tiles["hc", kk] = (hc, hs)
+
+        def zmm(i):
+            kk, half = divmod(i, 2)
+            hc, hs = tiles["hc", kk]
+            z = bank(2 + i % 4, [P, C], "z")
+            for g in range(2):
+                nc.tensor.matmul_mx(
+                    out=z[:],
+                    lhsT=hc[:, half, g * P : (g + 1) * P].bitcast(FP8X4),
+                    lhsT_scale=hs[:, half, g * P : (g + 1) * P],
+                    rhs=ww[:, g, :].bitcast(FP4X4),
+                    rhs_scale=ws[:, g, :],
+                    start=(g == 0),
+                    stop=(g == 1),
+                )
+            tiles["z", i] = z
+
+        def bymm(i):
+            q, j = divmod(i, 4)
+            t = bank(6 + i % 2, [P, C], "by")
+            nc.tensor.matmul(t[:], lhsT=dg[:, i, :], rhs=yt[q][:, j, :], start=True, stop=True)
+            tiles["by", i] = t
+
+        def absz(i):
+            kk, half = divmod(i, 2)
+            if half == 0:
+                tiles["az", kk] = work.tile([P, 2, C], F32, name="az", tag="az", bufs=2)
+            nc.scalar.activation(
+                out=tiles["az", kk][:, half, :], in_=tiles["z", i][:], func=ACT.Abs, accum_out=abs_acc[:, i : i + 1]
+            )
+
+        def sig(i):
+            s = work.tile([P, C], F32, name="s", tag="s", bufs=4)
+            nc.scalar.activation(out=s[:], in_=tiles["z", i][:], func=ACT.Sigmoid)
+            tiles["s", i] = s
+
+        def sigaz(kk):
+            u = work.tile([P, 2, C], F32, name="u", tag="u", bufs=2)
+            nc.scalar.activation(out=u[:], in_=tiles["az", kk][:], func=ACT.Sigmoid)
+            tiles["u", kk] = u
+
+        def yz(i):
+            q, j = divmod(i, 4)
+            junk = work.tile([P, C], BF16, name="junk", tag="junk", bufs=2)
+            nc.vector.scalar_tensor_tensor(
+                out=junk[:], in0=yt[q][:, j, :], scalar=0.5, in1=tiles["z", i][:],
+                op0=ALU.subtract, op1=ALU.mult, accum_out=yz_acc[:, i : i + 1],
+            )
+
+        def prod(kk):
+            nc.vector.tensor_reduce(
+                out=prods[:, 2 * kk : 2 * kk + 2, :], in_=tiles["u", kk][:].rearrange("p i (s e) -> p i s e", s=8),
+                axis=AX.X, op=ALU.mult,
+            )
+
+        def bdelta(i):
+            q, j = divmod(i, 4)
+            nc.vector.scalar_tensor_tensor(
+                out=bd[q][:, j, :], in0=tiles["s", i][:], scalar=b_col[:, i : i + 1], in1=tiles["by", i][:],
+                op0=ALU.mult, op1=ALU.subtract,
+            )
+
+        wb = {}
+
+        def wh_tile(q):
+            if q not in wb:
+                wb[q] = work.tile([P, 2, 4, P, 4], BF16, name="wb", tag="wb", bufs=4, align_bytes=64)
+            return wb[q]
+
+        def x_view(q, g, t0, tn):
+            return x[q][:].rearrange("p j (g m t) -> p g t m j", g=2, t=4)[:, g, t0 : t0 + tn]
+
+        def wh_vector(q, g, tp):
+            nc.vector.tensor_tensor(
+                out=wh_tile(q)[:, g, 2 * tp : 2 * tp + 2], in0=x_view(q, g, 2 * tp, 2),
+                in1=a_bf[:, q, :].unsqueeze(1).unsqueeze(1).to_broadcast([P, 2, P, 4]), op=ALU.mult,
+            )
+
+        def wh_gpsimd(q, g, tp):
+            for t in (2 * tp, 2 * tp + 1):
+                for m0 in (0, 64):
+                    nc.gpsimd.tensor_tensor(
+                        out=wh_tile(q)[:, g, t, m0 : m0 + 64, :], in0=x_view(q, g, t, 1)[:, 0, m0 : m0 + 64, :],
+                        in1=a_bf[:, q, :].unsqueeze(1).to_broadcast([P, 64, 4]), op=ALU.mult,
+                    )
+
+        def wquant(q):
+            nc.vector.quantize_mx(
+                out=w_codes[q][:].bitcast(FP8X4), scales=w_planes[q][:],
+                in_=wh_tile(q)[:].rearrange("p g t m j -> p (g t m j)"),
+            )
+
+        pairs = TILES // 2
+        for q in range(PASSES):
+            for g in range(2):
+                for tp in range(2):
+                    if (q, g, tp) not in V_PIECES:
+                        wh_gpsimd(q, g, tp)
+
+        for t in range(2):
+            tr(t)
+        for kk in range(pairs):
+            a, b2 = 2 * kk, 2 * kk + 1
+            last_a, last_b = a - 2, a - 1
+            copy(a)
+            copy(b2)
+            if kk == 0:
+                for i in range(4):
+                    diag_b(i)
+            if kk >= 2:
+                prod(kk - 2)
+            quant(kk)
+            for piece, step in V_PIECES.items():
+                if step == kk:
+                    wh_vector(*piece)
+            if kk == 0:
+                for i in range(4, TILES):
+                    diag_b(i)
+            if kk == 2:
+                weights()
+            if kk >= 1:
+                bymm(last_a)
+                bymm(last_b)
+            if kk + 1 < pairs:
+                tr(a + 2)
+                tr(a + 3)
+            zmm(a)
+            zmm(b2)
+            if kk >= 1:
+                absz(last_a)
+                sig(last_a)
+                absz(last_b)
+                sig(last_b)
+                sigaz(kk - 1)
+                yz(last_a)
+                bdelta(last_a)
+                if kk in WQ_STEPS:
+                    wquant(WQ_STEPS[kk])
+                yz(last_b)
+                bdelta(last_b)
+
+        bymm(TILES - 2)
+        bymm(TILES - 1)
+        absz(TILES - 2)
+        absz(TILES - 1)
+        sigaz(pairs - 1)
+        sig(TILES - 2)
+        sig(TILES - 1)
+        prod(pairs - 2)
+        yz(TILES - 2)
+        yz(TILES - 1)
+        prod(pairs - 1)
+        lnp = keep.tile([P, TILES, 8], F32, name="lnp")
+        nc.scalar.activation(out=lnp[:], in_=prods[:], func=ACT.Ln)
+        bdelta(TILES - 2)
+        lin = keep.tile([P, TILES], F32, name="lin")
+        lnu = keep.tile([P, TILES], F32, name="lnu")
+        nc.vector.tensor_reduce(out=lnu[:], in_=lnp[:], axis=AX.X, op=ALU.add)
+        nc.vector.scalar_tensor_tensor(
+            out=lin[:], in0=abs_acc[:], scalar=-0.5, in1=yz_acc[:], op0=ALU.mult, op1=ALU.add
+        )
+        rhs1 = keep.tile([P, 2, TILES], F32, name="rhs1")
+        rhs2 = keep.tile([P, 2, TILES], F32, name="rhs2")
+        nc.vector.tensor_tensor(
+            out=rhs2[:], in0=lnu[:].unsqueeze(1).to_broadcast([P, 2, TILES]), in1=wm[:], op=ALU.mult
+        )
+        nc.vector.tensor_tensor(
+            out=rhs1[:], in0=lin[:].unsqueeze(1).to_broadcast([P, 2, TILES]), in1=wm[:], op=ALU.mult
+        )
+        rhs1_first = rhs1[0:1].rearrange("o e (q j) -> o e q j", j=4)[:, :, :, 0]
+        nc.vector.scalar_tensor_tensor(
+            out=rhs1_first, in0=adj_bf[:].rearrange("o (q e) -> o e q", e=2), scalar=-0.125, in1=rhs1_first,
+            op0=ALU.mult, op1=ALU.add,
+        )
+        nv_bank = bank(0, [P, 2 * TILES], "nv")
+        nc.tensor.matmul(nv_bank[:], lhsT=ones[:], rhs=rhs2[:].rearrange("p e i -> p (e i)"), start=True, stop=False)
+        nc.tensor.matmul(nv_bank[:], lhsT=ones[:], rhs=rhs1[:].rearrange("p e i -> p (e i)"), start=False, stop=True)
+        nv = keep.tile([P, N_GROUPS], F32, name="nv")
+        nc.vector.tensor_reduce(
+            out=nv[:], in_=nv_bank[:].rearrange("p (g j) -> p g j", j=4), axis=AX.X, op=ALU.add
+        )
+        nmax = keep.tile([P, 1], F32, name="nmax")
+        nc.vector.tensor_reduce(out=nmax[:], in_=nv[:], axis=AX.X, op=ALU.min)
+        e = keep.tile([P, N_GROUPS], F32, name="e")
+        esum = keep.tile([P, 1], F32, name="esum")
+        nc.scalar.activation(out=e[:], in_=nv[:], func=ACT.Exp, scale=-1.0, bias=nmax[:], accum_out=esum[:])
+        bdelta(TILES - 1)
+        rinv = keep.tile([P, 1], F32, name="rinv")
+        nc.vector.reciprocal(out=rinv[:], in_=esum[:])
+        qv = keep.tile([P, PASSES], F32, name="qv")
+        for half in range(2):
+            rows = slice(64 * half, 64 * half + 64)
+            nc.vector.tensor_scalar(
+                out=qv[rows, :], in0=e[rows, 4 * half : 4 * half + 4], scalar1=rinv[rows, :], scalar2=None, op0=ALU.mult
+            )
+
+        dl = {}
+
+        def delta(q, ha):
+            t = work.tile([P, KH, 4], BF16, name="dl", tag="dl", bufs=4, align_bytes=64)
+            src = bd[q][:, :, ha * KH : (ha + 1) * KH].rearrange("p j k -> p k j")
+            nc.vector.tensor_scalar(
+                out=t[:, :V_COLS, :], in0=src[:, :V_COLS, :], scalar1=qv[:, q : q + 1], scalar2=None, op0=ALU.mult
+            )
+            nc.scalar.activation(out=t[:, V_COLS:, :], in_=src[:, V_COLS:, :], func=ACT.Copy, scale=qv[:, q : q + 1])
+            dl[q, ha] = t
+
+        def dquant(q, ha):
+            cols = slice(ha * KH, (ha + 1) * KH)
+            nc.vector.quantize_mx(
+                out=d_codes[q][:, cols].bitcast(FP8X4), scales=d_planes[q][:, cols],
+                in_=dl[q, ha][:].rearrange("p k j -> p (k j)"),
+            )
+
+        def gmm(out, q, g, t, ha):
+            sl = slice(g * C + t * P, g * C + (t + 1) * P)
+            cols = slice(ha * KH, (ha + 1) * KH)
+            nc.tensor.matmul_mx(
+                out=out,
+                lhsT=w_codes[q][:, sl].bitcast(FP8X4),
+                lhsT_scale=w_planes[q][:, sl],
+                rhs=d_codes[q][:, cols].bitcast(FP8X4),
+                rhs_scale=d_planes[q][:, cols],
+                start=(q == 0),
+                stop=(q == PASSES - 1),
+            )
+
+        delta(0, 0)
+        delta(1, 0)
+        dquant(0, 0)
+        delta(2, 0)
+        dquant(1, 0)
+        delta(3, 0)
+        dquant(2, 0)
+        wquant(3)
+        dquant(3, 0)
+        delta(0, 1)
+        delta(1, 1)
+        dquant(0, 1)
+        delta(2, 1)
+        dquant(1, 1)
+        delta(3, 1)
+        dquant(2, 1)
+        dquant(3, 1)
+
+        out_rows = out_0.rearrange("(g p t) k -> g p t k", p=P, t=4)
+        osc = [keep.tile([P, C], U8, name="osc%d" % g, align_bytes=64) for g in range(2)]
+
+        def finish(g, ha, banks, stores):
+            cols = slice(ha * KH, (ha + 1) * KH)
+            of = keep.tile([P, 4, KH], F32, name="of_%d_%d" % (g, ha))
+            for t in range(4):
+                nc.scalar.activation(out=of[:, t, :], in_=banks[t][:], func=ACT.Copy, scale=c8[:, g, t : t + 1])
+            for t in range(0, 4, 4 // stores):
+                ts = slice(t, t + 4 // stores)
+                nc.sync.dma_start(out=out_rows[g][:, ts, cols], in_=of[:, ts, :])
+            ob = keep.tile([P, KH, 4], BF16, name="ob_%d_%d" % (g, ha), align_bytes=64)
+            oc = keep.tile([P, KH], U32, name="oc_%d_%d" % (g, ha), align_bytes=64)
+            nc.vector.tensor_copy(out=ob[:], in_=of[:].rearrange("p t k -> p k t"))
+            nc.vector.quantize_mx(
+                out=oc[:].bitcast(FP8X4), scales=osc[g][:, cols], in_=ob[:].rearrange("p k t -> p (k t)")
+            )
+            nc.sync.dma_start(
+                out=out_1[g].rearrange("p m t -> p (m t)")[:, 4 * ha * KH : 4 * (ha + 1) * KH].bitcast(I32),
+                in_=oc[:].bitcast(I32),
+            )
+
+        def scales_out(g):
+            for r in range(4):
+                eng = nc.sync if r % 2 else nc.scalar
+                eng.dma_start(
+                    out=out_2[g, 4 * r : 4 * r + 4, :].bitcast(I32), in_=osc[g][32 * r : 32 * r + 4, :].bitcast(I32)
+                )
+
+        ba = [bank(t, [P, KH], "ga") for t in range(8)]
+        for q in range(PASSES):
+            for t in range(8):
+                gmm(ba[t][:], q, t // 4, t % 4, 0)
+        finish(0, 0, ba[:4], 1)
+        finish(1, 0, ba[4:], 1)
+        bb = [bank(t, [P, KH], "gb") for t in range(4)]
+        for q in range(PASSES):
+            for t in range(4):
+                gmm(bb[t][:], q, 0, t, 1)
+        finish(0, 1, bb, 1)
+        scales_out(0)
+        bc = [bank(4 + t, [P, KH], "gb") for t in range(4)]
+        for t in range(4):
+            for q in range(PASSES):
+                gmm(bc[t][:], q, 1, t, 1)
+        finish(1, 1, bc, 2)
+        scales_out(1)

@@ -22,8 +22,28 @@ TILES = TOKENS // P
 FLOPS = 2 * (2 * TOKENS * D * C)
 KH = 256
 V_COLS = 128
-V_PIECES = {(0, 1, 0): 0, (0, 1, 1): 1, (0, 0, 1): 1}
-WQ_STEPS = {3: 0, 5: 1, 7: 2}
+V1 = {
+    0: [("a", 0), ("a", 1), ("a", 2), ("a", 3)],
+    1: [("v", 0, 0, 0), ("v", 0, 1, 0)],
+    2: [("a", 4), ("a", 5)],
+    3: [("a", 6), ("a", 7)],
+    4: [("a", 8), ("a", 9), ("v", 1, 0, 0)],
+    5: [("a", 10), ("a", 11)],
+    6: [("a", 12), ("v", 2, 0, 0)],
+    7: [("a", 13), ("a", 14), ("a", 15)],
+}
+V2 = {
+    2: [("w", 0)],
+    4: [("v", 1, 1, 0)],
+    5: [("w", 1)],
+    6: [("v", 2, 1, 0)],
+    7: [("w", 2)],
+}
+S1 = {
+    1: [("s", 0, 0, 1), ("s", 0, 1, 1)],
+    4: [("s", 1, 0, 1), ("s", 1, 1, 1)],
+    6: [("s", 2, 0, 1), ("s", 2, 1, 1)],
+}
 
 
 def tile_groupdrologsumexppreconditionedgradient_x2_kernel(
@@ -202,42 +222,41 @@ def tile_groupdrologsumexppreconditionedgradient_x2_kernel(
                 op0=ALU.mult, op1=ALU.subtract,
             )
 
+        xs = {}
         wb = {}
 
-        def wh_tile(q):
-            if q not in wb:
-                wb[q] = work.tile([P, 2, 4, P, 4], BF16, name="wb", tag="wb", bufs=4, align_bytes=64)
-            return wb[q]
-
-        def x_view(q, g, t0, tn):
-            return x[q][:].rearrange("p j (g m t) -> p g t m j", g=2, t=4)[:, g, t0 : t0 + tn]
-
-        def wh_vector(q, g, tp):
-            nc.vector.tensor_tensor(
-                out=wh_tile(q)[:, g, 2 * tp : 2 * tp + 2], in0=x_view(q, g, 2 * tp, 2),
-                in1=a_bf[:, q, :].unsqueeze(1).unsqueeze(1).to_broadcast([P, 2, P, 4]), op=ALU.mult,
+        def amult(i):
+            q, j = divmod(i, 4)
+            if j == 0:
+                xs[q] = work.tile([P, 4, D], BF16, name="xs", tag="xs", bufs=2)
+                wb[q] = work.tile([P, 2, 4, P, 4], BF16, name="wb", tag="wb", bufs=2, align_bytes=64)
+            nc.vector.tensor_scalar(
+                out=xs[q][:, j, :], in0=x[q][:, j, :], scalar1=a_col[:, i : i + 1], scalar2=None, op0=ALU.mult
             )
 
-        def wh_gpsimd(q, g, tp):
-            for t in (2 * tp, 2 * tp + 1):
-                for m0 in (0, 64):
-                    nc.gpsimd.tensor_tensor(
-                        out=wh_tile(q)[:, g, t, m0 : m0 + 64, :], in0=x_view(q, g, t, 1)[:, 0, m0 : m0 + 64, :],
-                        in1=a_bf[:, q, :].unsqueeze(1).to_broadcast([P, 64, 4]), op=ALU.mult,
-                    )
+        def inter(q, g, tp, eng):
+            copy_fn = nc.vector.tensor_copy if eng == "v" else nc.scalar.copy
+            copy_fn(
+                out=wb[q][:, g, 2 * tp : 2 * tp + 2],
+                in_=xs[q][:].rearrange("p j (g m t) -> p g t m j", g=2, t=4)[:, g, 2 * tp : 2 * tp + 2],
+            )
 
         def wquant(q):
             nc.vector.quantize_mx(
                 out=w_codes[q][:].bitcast(FP8X4), scales=w_planes[q][:],
-                in_=wh_tile(q)[:].rearrange("p g t m j -> p (g t m j)"),
+                in_=wb[q][:].rearrange("p g t m j -> p (g t m j)"),
             )
 
         pairs = TILES // 2
-        for q in range(PASSES):
-            for g in range(2):
-                for tp in range(2):
-                    if (q, g, tp) not in V_PIECES:
-                        wh_gpsimd(q, g, tp)
+
+        def run(f):
+            kind = f[0]
+            if kind == "a":
+                amult(f[1])
+            elif kind == "w":
+                wquant(f[1])
+            else:
+                inter(f[1], f[2], f[3], kind)
 
         for t in range(2):
             tr(t)
@@ -252,9 +271,8 @@ def tile_groupdrologsumexppreconditionedgradient_x2_kernel(
             if kk >= 2:
                 prod(kk - 2)
             quant(kk)
-            for piece, step in V_PIECES.items():
-                if step == kk:
-                    wh_vector(*piece)
+            for f in V1.get(kk, []):
+                run(f)
             if kk == 0:
                 for i in range(4, TILES):
                     diag_b(i)
@@ -276,8 +294,11 @@ def tile_groupdrologsumexppreconditionedgradient_x2_kernel(
                 sigaz(kk - 1)
                 yz(last_a)
                 bdelta(last_a)
-                if kk in WQ_STEPS:
-                    wquant(WQ_STEPS[kk])
+            for f in S1.get(kk, []):
+                run(f)
+            for f in V2.get(kk, []):
+                run(f)
+            if kk >= 1:
                 yz(last_b)
                 bdelta(last_b)
 
@@ -321,11 +342,14 @@ def tile_groupdrologsumexppreconditionedgradient_x2_kernel(
         nc.vector.tensor_reduce(
             out=nv[:], in_=nv_bank[:].rearrange("p (g j) -> p g j", j=4), axis=AX.X, op=ALU.add
         )
+        run(("v", 3, 0, 0))
         nmax = keep.tile([P, 1], F32, name="nmax")
         nc.vector.tensor_reduce(out=nmax[:], in_=nv[:], axis=AX.X, op=ALU.min)
         e = keep.tile([P, N_GROUPS], F32, name="e")
         esum = keep.tile([P, 1], F32, name="esum")
         nc.scalar.activation(out=e[:], in_=nv[:], func=ACT.Exp, scale=-1.0, bias=nmax[:], accum_out=esum[:])
+        run(("s", 3, 0, 1))
+        run(("v", 3, 1, 0))
         bdelta(TILES - 1)
         rinv = keep.tile([P, 1], F32, name="rinv")
         nc.vector.reciprocal(out=rinv[:], in_=esum[:])
@@ -368,6 +392,7 @@ def tile_groupdrologsumexppreconditionedgradient_x2_kernel(
             )
 
         delta(0, 0)
+        run(("s", 3, 1, 1))
         delta(1, 0)
         dquant(0, 0)
         delta(2, 0)

@@ -22,28 +22,10 @@ TILES = TOKENS // P
 FLOPS = 2 * (2 * TOKENS * D * C)
 KH = 256
 V_COLS = 128
-V1 = {
-    0: [("a", 0), ("a", 1), ("a", 2), ("a", 3)],
-    1: [("v", 0, 0, 0), ("v", 0, 1, 0)],
-    2: [("a", 4), ("a", 5)],
-    3: [("a", 6), ("a", 7)],
-    4: [("a", 8), ("a", 9), ("v", 1, 0, 0)],
-    5: [("a", 10), ("a", 11)],
-    6: [("a", 12), ("v", 2, 0, 0)],
-    7: [("a", 13), ("a", 14), ("a", 15)],
-}
-V2 = {
-    2: [("w", 0)],
-    4: [("v", 1, 1, 0)],
-    5: [("w", 1)],
-    6: [("v", 2, 1, 0)],
-    7: [("w", 2)],
-}
-S1 = {
-    1: [("s", 0, 0, 1), ("s", 0, 1, 1)],
-    4: [("s", 1, 0, 1), ("s", 1, 1, 1)],
-    6: [("s", 2, 0, 1), ("s", 2, 1, 1)],
-}
+S_Q = 4
+S_3 = 2
+WARM1 = 0
+WARM2 = 0
 
 
 def tile_groupdrologsumexppreconditionedgradient_x2_kernel(
@@ -87,18 +69,19 @@ def tile_groupdrologsumexppreconditionedgradient_x2_kernel(
         y_rows = y.rearrange("g n k -> (g n) k").rearrange("(q p j) k -> q p j k", p=P, j=4)
         nc.vector.memset(ws[:].rearrange("p g n -> p (g n)").bitcast(I32), 0)
         make_identity(nc, ident_f[:])
-        nc.gpsimd.dma_start(out=b_bf[:], in_=b.rearrange("g n -> (g n)").rearrange("(q p j) -> p q j", p=P, j=4))
-        nc.gpsimd.dma_start(out=a_bf[:], in_=a.rearrange("g n -> (g n)").rearrange("(q p j) -> p q j", p=P, j=4))
         nc.sync.dma_start(out=x[0][:, 0, :], in_=h_rows[0][:, 0, :])
+        nc.sync.dma_start(out=x[0][:, 1, :], in_=h_rows[0][:, 1, :])
+        nc.sync.dma_start(out=ww[:].bitcast(I32), in_=w_words.rearrange("g p n -> p g n").bitcast(I32))
+        nc.sync.dma_start(out=x[0][:, 2, :], in_=h_rows[0][:, 2, :])
         for q in range(4):
             nc.scalar.dma_start(
                 out=ws[32 * q : 32 * q + 4, :, :].bitcast(I32),
                 in_=w_scales[:, 4 * q : 4 * q + 4, :].rearrange("g r n -> r g n").bitcast(I32),
             )
-        nc.sync.dma_start(out=ww[:].bitcast(I32), in_=w_words.rearrange("g p n -> p g n").bitcast(I32))
-        for j in range(1, 4):
-            nc.sync.dma_start(out=x[0][:, j, :], in_=h_rows[0][:, j, :])
+        nc.sync.dma_start(out=x[0][:, 3, :], in_=h_rows[0][:, 3, :])
+        nc.sync.dma_start(out=b_bf[:], in_=b.rearrange("g n -> (g n)").rearrange("(q p j) -> p q j", p=P, j=4))
         nc.sync.dma_start(out=yt[0][:], in_=y_rows[0])
+        nc.sync.dma_start(out=a_bf[:], in_=a.rearrange("g n -> (g n)").rearrange("(q p j) -> p q j", p=P, j=4))
         nc.gpsimd.dma_start(out=adj_bf[:], in_=adj.rearrange("(o g) -> o g", o=1))
         nc.gpsimd.dma_start(out=c_bf[:], in_=c.rearrange("(g p t) -> p g t", p=P, t=4))
         for q in range(1, PASSES):
@@ -144,32 +127,27 @@ def tile_groupdrologsumexppreconditionedgradient_x2_kernel(
             tiles["tr", i] = t
 
         def copy(i):
-            kk, half = divmod(i, 2)
-            if half == 0:
-                tiles["hq", kk] = work.tile([P, 2, D], BF16, name="hq", tag="hq", bufs=2, align_bytes=64)
+            hq = work.tile([P, D], BF16, name="hq", tag="hq", bufs=3, align_bytes=64)
             nc.scalar.copy(
-                out=tiles["hq", kk][:, half, :].bitcast(F32).rearrange("p (g r u) -> p g r u", g=2, u=2),
+                out=hq[:].bitcast(F32).rearrange("p (g r u) -> p g r u", g=2, u=2),
                 in_=tiles["tr", i][:].rearrange("p g u r -> p g r u"),
             )
+            tiles["hq", i] = hq
 
-        def quant(kk):
-            hc = work.tile([P, 2, 256], U32, name="hc", tag="hc", bufs=2, align_bytes=64)
-            hs = work.tile([P, 2, 256], U8, name="hs", tag="hs", bufs=2, align_bytes=64)
-            nc.vector.quantize_mx(
-                out=hc[:].rearrange("p i w -> p (i w)").bitcast(FP8X4), scales=hs[:].rearrange("p i w -> p (i w)"),
-                in_=tiles["hq", kk][:].rearrange("p i d -> p (i d)"),
-            )
-            tiles["hc", kk] = (hc, hs)
+        def quant(i):
+            hc = work.tile([P, 256], U32, name="hc", tag="hc", bufs=3, align_bytes=64)
+            hs = work.tile([P, 256], U8, name="hs", tag="hs", bufs=3, align_bytes=64)
+            nc.vector.quantize_mx(out=hc[:].bitcast(FP8X4), scales=hs[:], in_=tiles["hq", i][:])
+            tiles["hc", i] = (hc, hs)
 
         def zmm(i):
-            kk, half = divmod(i, 2)
-            hc, hs = tiles["hc", kk]
+            hc, hs = tiles["hc", i]
             z = bank(2 + i % 4, [P, C], "z")
             for g in range(2):
                 nc.tensor.matmul_mx(
                     out=z[:],
-                    lhsT=hc[:, half, g * P : (g + 1) * P].bitcast(FP8X4),
-                    lhsT_scale=hs[:, half, g * P : (g + 1) * P],
+                    lhsT=hc[:, g * P : (g + 1) * P].bitcast(FP8X4),
+                    lhsT_scale=hs[:, g * P : (g + 1) * P],
                     rhs=ww[:, g, :].bitcast(FP4X4),
                     rhs_scale=ws[:, g, :],
                     start=(g == 0),
@@ -184,22 +162,19 @@ def tile_groupdrologsumexppreconditionedgradient_x2_kernel(
             tiles["by", i] = t
 
         def absz(i):
-            kk, half = divmod(i, 2)
-            if half == 0:
-                tiles["az", kk] = work.tile([P, 2, C], F32, name="az", tag="az", bufs=2)
-            nc.scalar.activation(
-                out=tiles["az", kk][:, half, :], in_=tiles["z", i][:], func=ACT.Abs, accum_out=abs_acc[:, i : i + 1]
-            )
+            az = work.tile([P, C], F32, name="az", tag="az", bufs=2)
+            nc.scalar.activation(out=az[:], in_=tiles["z", i][:], func=ACT.Abs, accum_out=abs_acc[:, i : i + 1])
+            tiles["az", i] = az
 
         def sig(i):
             s = work.tile([P, C], F32, name="s", tag="s", bufs=4)
             nc.scalar.activation(out=s[:], in_=tiles["z", i][:], func=ACT.Sigmoid)
             tiles["s", i] = s
 
-        def sigaz(kk):
-            u = work.tile([P, 2, C], F32, name="u", tag="u", bufs=2)
-            nc.scalar.activation(out=u[:], in_=tiles["az", kk][:], func=ACT.Sigmoid)
-            tiles["u", kk] = u
+        def sigaz(i):
+            u = work.tile([P, C], F32, name="u", tag="u", bufs=3)
+            nc.scalar.activation(out=u[:], in_=tiles["az", i][:], func=ACT.Sigmoid)
+            tiles["u", i] = u
 
         def yz(i):
             q, j = divmod(i, 4)
@@ -209,10 +184,9 @@ def tile_groupdrologsumexppreconditionedgradient_x2_kernel(
                 op0=ALU.subtract, op1=ALU.mult, accum_out=yz_acc[:, i : i + 1],
             )
 
-        def prod(kk):
+        def prod(i):
             nc.vector.tensor_reduce(
-                out=prods[:, 2 * kk : 2 * kk + 2, :], in_=tiles["u", kk][:].rearrange("p i (s e) -> p i s e", s=8),
-                axis=AX.X, op=ALU.mult,
+                out=prods[:, i, :], in_=tiles["u", i][:].rearrange("p (s e) -> p s e", s=8), axis=AX.X, op=ALU.mult
             )
 
         def bdelta(i):
@@ -228,94 +202,95 @@ def tile_groupdrologsumexppreconditionedgradient_x2_kernel(
         def amult(i):
             q, j = divmod(i, 4)
             if j == 0:
-                xs[q] = work.tile([P, 4, D], BF16, name="xs", tag="xs", bufs=2)
-                wb[q] = work.tile([P, 2, 4, P, 4], BF16, name="wb", tag="wb", bufs=2, align_bytes=64)
+                xs[q] = work.tile([P, 4, D], BF16, name="xs", tag="xs", bufs=3)
+                wb[q] = work.tile([P, 2, 4, P, 4], BF16, name="wb", tag="wb", bufs=3, align_bytes=64)
             nc.vector.tensor_scalar(
                 out=xs[q][:, j, :], in0=x[q][:, j, :], scalar1=a_col[:, i : i + 1], scalar2=None, op0=ALU.mult
             )
 
-        def inter(q, g, tp, eng):
+        def inter(q, g, eng, m0, mn):
             copy_fn = nc.vector.tensor_copy if eng == "v" else nc.scalar.copy
+            ms = slice(m0, m0 + mn)
             copy_fn(
-                out=wb[q][:, g, 2 * tp : 2 * tp + 2],
-                in_=xs[q][:].rearrange("p j (g m t) -> p g t m j", g=2, t=4)[:, g, 2 * tp : 2 * tp + 2],
+                out=wb[q][:, g].rearrange("p t m j -> p m t j")[:, ms],
+                in_=xs[q][:, :, g * C : (g + 1) * C].rearrange("p j (m t) -> p m t j", t=4)[:, ms],
             )
 
-        def wquant(q):
+        def wquant(q, g):
+            cols = slice(g * C, (g + 1) * C)
             nc.vector.quantize_mx(
-                out=w_codes[q][:].bitcast(FP8X4), scales=w_planes[q][:],
-                in_=wb[q][:].rearrange("p g t m j -> p (g t m j)"),
+                out=w_codes[q][:, cols].bitcast(FP8X4), scales=w_planes[q][:, cols],
+                in_=wb[q][:, g].rearrange("p t m j -> p (t m j)"),
             )
 
-        pairs = TILES // 2
+        v_c = {}
+        s_c = {}
 
-        def run(f):
-            kind = f[0]
-            if kind == "a":
-                amult(f[1])
-            elif kind == "w":
-                wquant(f[1])
-            else:
-                inter(f[1], f[2], f[3], kind)
+        def at(table, step, f, *args):
+            table.setdefault(step, []).append(lambda: f(*args))
 
-        for t in range(2):
-            tr(t)
-        for kk in range(pairs):
-            a, b2 = 2 * kk, 2 * kk + 1
-            last_a, last_b = a - 2, a - 1
-            copy(a)
-            copy(b2)
-            if kk == 0:
-                for i in range(4):
+        for i in range(TILES):
+            at(v_c, max(i, 2), amult, i)
+        for q in range(3):
+            for n in range(2):
+                at(v_c, 4 * q + 5 + n, inter, q, 0, "v", 64 * n, 64)
+            for n in range(S_Q):
+                at(s_c, 4 * q + 4 + n, inter, q, 1, "s", 32 * n, 32)
+            if S_Q < 4:
+                at(v_c, 4 * q + 7, inter, q, 1, "v", 32 * S_Q, 128 - 32 * S_Q)
+            if q < 2:
+                at(v_c, 4 * q + 8, wquant, q, 0)
+                at(v_c, 4 * q + 10, wquant, q, 1)
+        for n in range(S_3):
+            at(s_c, 16 - n // 2, inter, 3, 1, "s", 32 * n, 32)
+
+        for n in range(WARM1):
+            nc.tensor.matmul(bank(7, [P, P], "warm1")[:], lhsT=ident_b[:], rhs=ident_b[:], start=True, stop=True)
+        tr(0)
+        tr(1)
+        for k in range(TILES + 2):
+            if 2 <= k < TILES + 1:
+                absz(k - 2)
+                sig(k - 2)
+            if k < TILES:
+                copy(k)
+            if 2 <= k < TILES + 1:
+                sigaz(k - 2)
+            if k == TILES + 1:
+                absz(k - 2)
+                sigaz(k - 2)
+                sig(k - 2)
+            if 1 <= k < TILES + 1:
+                quant(k - 1)
+                zmm(k - 1)
+            if 3 <= k:
+                prod(k - 3)
+            if k + 2 < TILES:
+                tr(k + 2)
+            if 2 <= k:
+                bymm(k - 2)
+            for f in s_c.get(k, []):
+                f()
+            if 3 <= k:
+                yz(k - 3)
+            for f in v_c.get(k, []):
+                f()
+            if k == 1:
+                for i in range(TILES):
                     diag_b(i)
-            if kk >= 2:
-                prod(kk - 2)
-            quant(kk)
-            for f in V1.get(kk, []):
-                run(f)
-            if kk == 0:
-                for i in range(4, TILES):
-                    diag_b(i)
-            if kk == 2:
+            if k == 5:
                 weights()
-            if kk >= 1:
-                bymm(last_a)
-                bymm(last_b)
-            if kk + 1 < pairs:
-                tr(a + 2)
-                tr(a + 3)
-            zmm(a)
-            zmm(b2)
-            if kk >= 1:
-                absz(last_a)
-                sig(last_a)
-                absz(last_b)
-                sig(last_b)
-                sigaz(kk - 1)
-                yz(last_a)
-                bdelta(last_a)
-            for f in S1.get(kk, []):
-                run(f)
-            for f in V2.get(kk, []):
-                run(f)
-            if kk >= 1:
-                yz(last_b)
-                bdelta(last_b)
+            if 3 <= k:
+                bdelta(k - 3)
+        for f in v_c.get(TILES + 2, []):
+            f()
 
-        bymm(TILES - 2)
-        bymm(TILES - 1)
-        absz(TILES - 2)
-        absz(TILES - 1)
-        sigaz(pairs - 1)
-        sig(TILES - 2)
-        sig(TILES - 1)
-        prod(pairs - 2)
-        yz(TILES - 2)
+        prod(TILES - 1)
         yz(TILES - 1)
-        prod(pairs - 1)
         lnp = keep.tile([P, TILES, 8], F32, name="lnp")
         nc.scalar.activation(out=lnp[:], in_=prods[:], func=ACT.Ln)
-        bdelta(TILES - 2)
+        wquant(2, 0)
+        wquant(2, 1)
         lin = keep.tile([P, TILES], F32, name="lin")
         lnu = keep.tile([P, TILES], F32, name="lnu")
         nc.vector.tensor_reduce(out=lnu[:], in_=lnp[:], axis=AX.X, op=ALU.add)
@@ -338,18 +313,16 @@ def tile_groupdrologsumexppreconditionedgradient_x2_kernel(
         nv_bank = bank(0, [P, 2 * TILES], "nv")
         nc.tensor.matmul(nv_bank[:], lhsT=ones[:], rhs=rhs2[:].rearrange("p e i -> p (e i)"), start=True, stop=False)
         nc.tensor.matmul(nv_bank[:], lhsT=ones[:], rhs=rhs1[:].rearrange("p e i -> p (e i)"), start=False, stop=True)
+        inter(3, 0, "v", 0, 64)
         nv = keep.tile([P, N_GROUPS], F32, name="nv")
         nc.vector.tensor_reduce(
             out=nv[:], in_=nv_bank[:].rearrange("p (g j) -> p g j", j=4), axis=AX.X, op=ALU.add
         )
-        run(("v", 3, 0, 0))
         nmax = keep.tile([P, 1], F32, name="nmax")
         nc.vector.tensor_reduce(out=nmax[:], in_=nv[:], axis=AX.X, op=ALU.min)
         e = keep.tile([P, N_GROUPS], F32, name="e")
         esum = keep.tile([P, 1], F32, name="esum")
         nc.scalar.activation(out=e[:], in_=nv[:], func=ACT.Exp, scale=-1.0, bias=nmax[:], accum_out=esum[:])
-        run(("s", 3, 0, 1))
-        run(("v", 3, 1, 0))
         bdelta(TILES - 1)
         rinv = keep.tile([P, 1], F32, name="rinv")
         nc.vector.reciprocal(out=rinv[:], in_=esum[:])
@@ -360,10 +333,17 @@ def tile_groupdrologsumexppreconditionedgradient_x2_kernel(
                 out=qv[rows, :], in0=e[rows, 4 * half : 4 * half + 4], scalar1=rinv[rows, :], scalar2=None, op0=ALU.mult
             )
 
+        for n in range(WARM2):
+            hc, hs = tiles["hc", TILES - 1]
+            nc.tensor.matmul_mx(
+                out=bank(7, [P, C], "warm2")[:], lhsT=hc[:, 0:P].bitcast(FP8X4), lhsT_scale=hs[:, 0:P],
+                rhs=ww[:, 0, :].bitcast(FP4X4), rhs_scale=ws[:, 0, :], start=True, stop=True,
+            )
+
         dl = {}
 
         def delta(q, ha):
-            t = work.tile([P, KH, 4], BF16, name="dl", tag="dl", bufs=4, align_bytes=64)
+            t = work.tile([P, KH, 4], BF16, name="dl", tag="dl", bufs=3, align_bytes=64)
             src = bd[q][:, :, ha * KH : (ha + 1) * KH].rearrange("p j k -> p k j")
             nc.vector.tensor_scalar(
                 out=t[:, :V_COLS, :], in0=src[:, :V_COLS, :], scalar1=qv[:, q : q + 1], scalar2=None, op0=ALU.mult
@@ -392,14 +372,17 @@ def tile_groupdrologsumexppreconditionedgradient_x2_kernel(
             )
 
         delta(0, 0)
-        run(("s", 3, 1, 1))
         delta(1, 0)
         dquant(0, 0)
         delta(2, 0)
         dquant(1, 0)
         delta(3, 0)
         dquant(2, 0)
-        wquant(3)
+        inter(3, 0, "v", 64, 64)
+        if S_3 < 4:
+            inter(3, 1, "v", 32 * S_3, 128 - 32 * S_3)
+        wquant(3, 0)
+        wquant(3, 1)
         dquant(3, 0)
         delta(0, 1)
         delta(1, 1)
@@ -415,13 +398,13 @@ def tile_groupdrologsumexppreconditionedgradient_x2_kernel(
 
         def finish(g, ha, banks, stores):
             cols = slice(ha * KH, (ha + 1) * KH)
-            of = keep.tile([P, 4, KH], F32, name="of_%d_%d" % (g, ha))
+            of = work.tile([P, 4, KH], F32, name="of", tag="of", bufs=4)
             for t in range(4):
                 nc.scalar.activation(out=of[:, t, :], in_=banks[t][:], func=ACT.Copy, scale=c8[:, g, t : t + 1])
             for t in range(0, 4, 4 // stores):
                 ts = slice(t, t + 4 // stores)
                 nc.sync.dma_start(out=out_rows[g][:, ts, cols], in_=of[:, ts, :])
-            ob = keep.tile([P, KH, 4], BF16, name="ob_%d_%d" % (g, ha), align_bytes=64)
+            ob = work.tile([P, KH, 4], BF16, name="ob", tag="ob", bufs=2, align_bytes=64)
             oc = keep.tile([P, KH], U32, name="oc_%d_%d" % (g, ha), align_bytes=64)
             nc.vector.tensor_copy(out=ob[:], in_=of[:].rearrange("p t k -> p k t"))
             nc.vector.quantize_mx(
@@ -434,7 +417,7 @@ def tile_groupdrologsumexppreconditionedgradient_x2_kernel(
 
         def scales_out(g):
             for r in range(4):
-                eng = nc.sync if r % 2 else nc.scalar
+                eng = nc.gpsimd if g == 0 else nc.sync if r % 2 else nc.scalar
                 eng.dma_start(
                     out=out_2[g, 4 * r : 4 * r + 4, :].bitcast(I32), in_=osc[g][32 * r : 32 * r + 4, :].bitcast(I32)
                 )

@@ -22,9 +22,7 @@ TILES = TOKENS // P
 FLOPS = 2 * (2 * TOKENS * D * C)
 KH = 256
 V_COLS = 128
-S_Q = 4
-S_3 = 2
-WARM1 = 0
+WARM1 = 10
 WARM2 = 0
 
 
@@ -208,12 +206,11 @@ def tile_groupdrologsumexppreconditionedgradient_x2_kernel(
                 out=xs[q][:, j, :], in0=x[q][:, j, :], scalar1=a_col[:, i : i + 1], scalar2=None, op0=ALU.mult
             )
 
-        def inter(q, g, eng, m0, mn):
+        def inter(q, g, tp, eng, m0, mn):
             copy_fn = nc.vector.tensor_copy if eng == "v" else nc.scalar.copy
-            ms = slice(m0, m0 + mn)
             copy_fn(
-                out=wb[q][:, g].rearrange("p t m j -> p m t j")[:, ms],
-                in_=xs[q][:, :, g * C : (g + 1) * C].rearrange("p j (m t) -> p m t j", t=4)[:, ms],
+                out=wb[q][:, g, 2 * tp : 2 * tp + 2, m0 : m0 + mn, :].rearrange("p t m j -> p m t j"),
+                in_=xs[q][:, :, g * C : (g + 1) * C].rearrange("p j (m t) -> p m t j", t=4)[:, m0 : m0 + mn, 2 * tp : 2 * tp + 2],
             )
 
         def wquant(q, g):
@@ -233,16 +230,14 @@ def tile_groupdrologsumexppreconditionedgradient_x2_kernel(
             at(v_c, max(i, 2), amult, i)
         for q in range(3):
             for n in range(2):
-                at(v_c, 4 * q + 5 + n, inter, q, 0, "v", 64 * n, 64)
-            for n in range(S_Q):
-                at(s_c, 4 * q + 4 + n, inter, q, 1, "s", 32 * n, 32)
-            if S_Q < 4:
-                at(v_c, 4 * q + 7, inter, q, 1, "v", 32 * S_Q, 128 - 32 * S_Q)
+                at(v_c, 4 * q + 5 + n, inter, q, 0, n, "v", 0, P)
+            for n in range(4):
+                at(s_c, 4 * q + 4 + n, inter, q, 1, n // 2, "s", 64 * (n % 2), 64)
             if q < 2:
                 at(v_c, 4 * q + 8, wquant, q, 0)
                 at(v_c, 4 * q + 10, wquant, q, 1)
-        for n in range(S_3):
-            at(s_c, 16 - n // 2, inter, 3, 1, "s", 32 * n, 32)
+        for n in range(2):
+            at(s_c, 16, inter, 3, 1, 0, "s", 64 * n, 64)
 
         for n in range(WARM1):
             nc.tensor.matmul(bank(7, [P, P], "warm1")[:], lhsT=ident_b[:], rhs=ident_b[:], start=True, stop=True)
@@ -313,7 +308,7 @@ def tile_groupdrologsumexppreconditionedgradient_x2_kernel(
         nv_bank = bank(0, [P, 2 * TILES], "nv")
         nc.tensor.matmul(nv_bank[:], lhsT=ones[:], rhs=rhs2[:].rearrange("p e i -> p (e i)"), start=True, stop=False)
         nc.tensor.matmul(nv_bank[:], lhsT=ones[:], rhs=rhs1[:].rearrange("p e i -> p (e i)"), start=False, stop=True)
-        inter(3, 0, "v", 0, 64)
+        inter(3, 0, 0, "v", 0, P)
         nv = keep.tile([P, N_GROUPS], F32, name="nv")
         nc.vector.tensor_reduce(
             out=nv[:], in_=nv_bank[:].rearrange("p (g j) -> p g j", j=4), axis=AX.X, op=ALU.add
@@ -378,9 +373,8 @@ def tile_groupdrologsumexppreconditionedgradient_x2_kernel(
         dquant(1, 0)
         delta(3, 0)
         dquant(2, 0)
-        inter(3, 0, "v", 64, 64)
-        if S_3 < 4:
-            inter(3, 1, "v", 32 * S_3, 128 - 32 * S_3)
+        inter(3, 0, 1, "v", 0, P)
+        inter(3, 1, 1, "v", 0, P)
         wquant(3, 0)
         wquant(3, 1)
         dquant(3, 0)
@@ -394,7 +388,15 @@ def tile_groupdrologsumexppreconditionedgradient_x2_kernel(
         dquant(3, 1)
 
         out_rows = out_0.rearrange("(g p t) k -> g p t k", p=P, t=4)
-        osc = [keep.tile([P, C], U8, name="osc%d" % g, align_bytes=64) for g in range(2)]
+        osc = keep.tile([P, 2, C], U8, name="osc", align_bytes=64)
+
+        def scales_out():
+            for r in range(4):
+                eng = nc.sync if r % 2 else nc.scalar
+                eng.dma_start(
+                    out=out_2[:, 4 * r : 4 * r + 4, :].rearrange("g r m -> r g m").bitcast(I32),
+                    in_=osc[32 * r : 32 * r + 4, :, :].bitcast(I32),
+                )
 
         def finish(g, ha, banks, stores):
             cols = slice(ha * KH, (ha + 1) * KH)
@@ -408,19 +410,12 @@ def tile_groupdrologsumexppreconditionedgradient_x2_kernel(
             oc = keep.tile([P, KH], U32, name="oc_%d_%d" % (g, ha), align_bytes=64)
             nc.vector.tensor_copy(out=ob[:], in_=of[:].rearrange("p t k -> p k t"))
             nc.vector.quantize_mx(
-                out=oc[:].bitcast(FP8X4), scales=osc[g][:, cols], in_=ob[:].rearrange("p k t -> p (k t)")
+                out=oc[:].bitcast(FP8X4), scales=osc[:, g, cols], in_=ob[:].rearrange("p k t -> p (k t)")
             )
             nc.sync.dma_start(
                 out=out_1[g].rearrange("p m t -> p (m t)")[:, 4 * ha * KH : 4 * (ha + 1) * KH].bitcast(I32),
                 in_=oc[:].bitcast(I32),
             )
-
-        def scales_out(g):
-            for r in range(4):
-                eng = nc.gpsimd if g == 0 else nc.sync if r % 2 else nc.scalar
-                eng.dma_start(
-                    out=out_2[g, 4 * r : 4 * r + 4, :].bitcast(I32), in_=osc[g][32 * r : 32 * r + 4, :].bitcast(I32)
-                )
 
         ba = [bank(t, [P, KH], "ga") for t in range(8)]
         for q in range(PASSES):
@@ -433,10 +428,9 @@ def tile_groupdrologsumexppreconditionedgradient_x2_kernel(
             for t in range(4):
                 gmm(bb[t][:], q, 0, t, 1)
         finish(0, 1, bb, 1)
-        scales_out(0)
         bc = [bank(4 + t, [P, KH], "gb") for t in range(4)]
         for t in range(4):
             for q in range(PASSES):
                 gmm(bc[t][:], q, 1, t, 1)
-        finish(1, 1, bc, 2)
-        scales_out(1)
+        finish(1, 1, bc, 1)
+        scales_out()

@@ -15,15 +15,22 @@ ALU = mybir.AluOpType
 AX = mybir.AxisListType
 
 N_GROUPS, N_EX, D, C = 8, 256, 1024, 512
-TOKENS = N_GROUPS * N_EX
+ETA = 0.125
 P = 128
-PASSES = TOKENS // 512
+PACK = 4
+STRETCH = P * PACK
+TOKENS = N_GROUPS * N_EX
+SPANS = TOKENS // STRETCH
 TILES = TOKENS // P
-FLOPS = 2 * (2 * TOKENS * D * C)
-KH = 256
+F_GROUPS = D // STRETCH
+HALF_C = C // 2
+FACTORS = 64
+
+LAG = 3
 V_COLS = 128
-WARM1 = 10
-WARM2 = 0
+LAST_SHARE = 64
+
+FLOPS = 2 * (2 * TOKENS * D * C)
 
 
 def tile_groupdrologsumexppreconditionedgradient_x2_kernel(
@@ -37,400 +44,383 @@ def tile_groupdrologsumexppreconditionedgradient_x2_kernel(
         ctx.enter_context(tc.manual_schedule())
 
         def bank(index, shape, what):
-            return psum.tile(shape, F32, name="%s_b%d" % (what, index), tag="bank%d" % index, bufs=1)
+            return psum.tile(shape, F32, name="%s_%d" % (what, index), tag="bank%d" % index, bufs=1)
 
-        x = [keep.tile([P, 4, D], BF16, name="x%d" % g) for g in range(PASSES)]
-        yt = [keep.tile([P, 4, C], BF16, name="y%d" % g) for g in range(PASSES)]
-        bd = [keep.tile([P, 4, C], F32, name="bd%d" % g) for g in range(PASSES)]
-        w_codes = [keep.tile([P, D], U32, name="wc%d" % g, align_bytes=64) for g in range(PASSES)]
-        w_planes = [keep.tile([P, D], U8, name="wp%d" % g, align_bytes=64) for g in range(PASSES)]
-        d_codes = [keep.tile([P, C], U32, name="dc%d" % g, align_bytes=64) for g in range(PASSES)]
-        d_planes = [keep.tile([P, C], U8, name="dp%d" % g, align_bytes=64) for g in range(PASSES)]
-        ww = keep.tile([P, 2, 2 * C], U8, name="ww", align_bytes=64)
-        ws = keep.tile([P, 2, C], U8, name="ws", align_bytes=64)
-        a_bf = keep.tile([P, PASSES, 4], BF16, name="a_bf")
-        b_bf = keep.tile([P, PASSES, 4], BF16, name="b_bf")
-        c_bf = keep.tile([P, 2, 4], BF16, name="c_bf")
-        adj_bf = keep.tile([1, N_GROUPS], BF16, name="adj_bf")
-        c8 = keep.tile([P, 2, 4], F32, name="c8")
-        wab = keep.tile([P, TILES], F32, name="wab")
-        wm = keep.tile([P, 2, TILES], F32, name="wm")
+        x = [keep.tile([P, 4, D], BF16, name="x%d" % s) for s in range(SPANS)]
+        y_in = [keep.tile([P, 4, C], BF16, name="y%d" % s) for s in range(SPANS)]
+        residual = [keep.tile([P, 4, C], F32, name="residual%d" % s) for s in range(SPANS)]
+        wh_codes = [keep.tile([P, D], U32, name="wh_codes%d" % s, align_bytes=64) for s in range(SPANS)]
+        wh_scales = [keep.tile([P, D], U8, name="wh_scales%d" % s, align_bytes=64) for s in range(SPANS)]
+        dl_codes = [keep.tile([P, C], U32, name="dl_codes%d" % s, align_bytes=64) for s in range(SPANS)]
+        dl_scales = [keep.tile([P, C], U8, name="dl_scales%d" % s, align_bytes=64) for s in range(SPANS)]
+        w_sb = keep.tile([P, F_GROUPS, 2 * C], U8, name="w_sb", align_bytes=64)
+        w_sc = keep.tile([P, F_GROUPS, C], U8, name="w_sc", align_bytes=64)
+        a_in = keep.tile([P, SPANS, 4], BF16, name="a_in")
+        b_in = keep.tile([P, SPANS, 4], BF16, name="b_in")
+        c_in = keep.tile([P, F_GROUPS, 4], BF16, name="c_in")
+        adj_in = keep.tile([1, N_GROUPS], BF16, name="adj_in")
+        out_factor = keep.tile([P, F_GROUPS, 4], F32, name="out_factor")
+        loss_weight = keep.tile([P, TILES], F32, name="loss_weight")
+        group_weight = keep.tile([P, 2, TILES], F32, name="group_weight")
         ones = keep.tile([P, P], F32, name="ones")
+        half = keep.tile([P, 1], F32, name="half")
         ident_f = keep.tile([P, P], F32, name="ident_f")
         ident_b = keep.tile([P, P], BF16, name="ident_b")
-        dg = keep.tile([P, TILES, P], BF16, name="dg")
-        abs_acc = keep.tile([P, TILES], F32, name="abs_acc")
-        yz_acc = keep.tile([P, TILES], F32, name="yz_acc")
-        prods = keep.tile([P, TILES, 8], F32, name="prods")
+        diag_b = keep.tile([P, TILES, P], BF16, name="diag_b")
+        abs_sum = keep.tile([P, TILES], F32, name="abs_sum")
+        yz_sum = keep.tile([P, TILES], F32, name="yz_sum")
+        products = keep.tile([P, TILES, C // FACTORS], F32, name="products")
 
-        h_rows = h.rearrange("g n d -> (g n) d").rearrange("(q p j) d -> q p j d", p=P, j=4)
-        y_rows = y.rearrange("g n k -> (g n) k").rearrange("(q p j) k -> q p j k", p=P, j=4)
-        nc.vector.memset(ws[:].rearrange("p g n -> p (g n)").bitcast(I32), 0)
+        h_rows = h.rearrange("g n d -> (g n) d").rearrange("(s p j) d -> s p j d", p=P, j=4)
+        y_rows = y.rearrange("g n k -> (g n) k").rearrange("(s p j) k -> s p j k", p=P, j=4)
+        nc.vector.memset(w_sc[:].rearrange("p g n -> p (g n)").bitcast(I32), 0)
         make_identity(nc, ident_f[:])
         nc.sync.dma_start(out=x[0][:, 0, :], in_=h_rows[0][:, 0, :])
         nc.sync.dma_start(out=x[0][:, 1, :], in_=h_rows[0][:, 1, :])
-        nc.sync.dma_start(out=ww[:].bitcast(I32), in_=w_words.rearrange("g p n -> p g n").bitcast(I32))
+        nc.sync.dma_start(out=w_sb[:].bitcast(I32), in_=w_words.rearrange("g p n -> p g n").bitcast(I32))
         nc.sync.dma_start(out=x[0][:, 2, :], in_=h_rows[0][:, 2, :])
-        for q in range(4):
+        for quad in range(4):
             nc.scalar.dma_start(
-                out=ws[32 * q : 32 * q + 4, :, :].bitcast(I32),
-                in_=w_scales[:, 4 * q : 4 * q + 4, :].rearrange("g r n -> r g n").bitcast(I32),
+                out=w_sc[32 * quad : 32 * quad + 4, :, :].bitcast(I32),
+                in_=w_scales[:, 4 * quad : 4 * quad + 4, :].rearrange("g r n -> r g n").bitcast(I32),
             )
         nc.sync.dma_start(out=x[0][:, 3, :], in_=h_rows[0][:, 3, :])
-        nc.sync.dma_start(out=b_bf[:], in_=b.rearrange("g n -> (g n)").rearrange("(q p j) -> p q j", p=P, j=4))
-        nc.sync.dma_start(out=yt[0][:], in_=y_rows[0])
-        nc.sync.dma_start(out=a_bf[:], in_=a.rearrange("g n -> (g n)").rearrange("(q p j) -> p q j", p=P, j=4))
-        nc.gpsimd.dma_start(out=adj_bf[:], in_=adj.rearrange("(o g) -> o g", o=1))
-        nc.gpsimd.dma_start(out=c_bf[:], in_=c.rearrange("(g p t) -> p g t", p=P, t=4))
-        for q in range(1, PASSES):
-            nc.sync.dma_start(out=x[q][:, 0:2, :], in_=h_rows[q][:, 0:2, :])
-            nc.sync.dma_start(out=x[q][:, 2:4, :], in_=h_rows[q][:, 2:4, :])
-            nc.sync.dma_start(out=yt[q][:], in_=y_rows[q])
+        nc.sync.dma_start(out=b_in[:], in_=b.rearrange("g n -> (g n)").rearrange("(s p j) -> p s j", p=P, j=4))
+        nc.sync.dma_start(out=y_in[0][:], in_=y_rows[0])
+        nc.sync.dma_start(out=a_in[:], in_=a.rearrange("g n -> (g n)").rearrange("(s p j) -> p s j", p=P, j=4))
+        nc.gpsimd.dma_start(out=adj_in[:], in_=adj.rearrange("(o g) -> o g", o=1))
+        nc.gpsimd.dma_start(out=c_in[:], in_=c.rearrange("(f p t) -> p f t", p=P, t=4))
+        for s in range(1, SPANS):
+            nc.sync.dma_start(out=x[s][:, 0:2, :], in_=h_rows[s][:, 0:2, :])
+            nc.sync.dma_start(out=x[s][:, 2:4, :], in_=h_rows[s][:, 2:4, :])
+            nc.sync.dma_start(out=y_in[s][:], in_=y_rows[s])
 
-        a_col = a_bf[:].rearrange("p q j -> p (q j)")
-        b_col = b_bf[:].rearrange("p q j -> p (q j)")
+        a_col = a_in[:].rearrange("p s j -> p (s j)")
+        b_col = b_in[:].rearrange("p s j -> p (s j)")
         nc.vector.tensor_copy(out=ident_b[:], in_=ident_f[:])
         nc.vector.memset(ones[:], 1.0)
-        warm = keep.tile([P, 1], F32, name="warm")
-        nc.scalar.activation(out=warm[:], in_=ones[:, 0:1], func=ACT.Sigmoid)
-        nc.vector.memset(wm[:], 0.0)
+        nc.vector.memset(half[:], 0.0)
+        nc.scalar.activation(out=half[:], in_=half[:], func=ACT.Sigmoid)
+        nc.vector.memset(group_weight[:], 0.0)
 
-        def diag_b(i):
-            nc.vector.tensor_scalar(
-                out=dg[:, i, :], in0=ident_b[:], scalar1=b_col[:, i : i + 1], scalar2=None, op0=ALU.mult
-            )
+        def diagonals_of_b():
+            for i in range(TILES):
+                nc.vector.tensor_scalar(
+                    out=diag_b[:, i, :], in0=ident_b[:], scalar1=b_col[:, i : i + 1], scalar2=None, op0=ALU.mult
+                )
 
-        def weights():
+        def loss_weights():
             nc.vector.scalar_tensor_tensor(
-                out=wab[:], in0=a_col, scalar=1.0 / 2048, in1=b_col, op0=ALU.mult, op1=ALU.mult
+                out=loss_weight[:], in0=a_col, scalar=ETA / N_EX, in1=b_col, op0=ALU.mult, op1=ALU.mult
             )
             nc.vector.tensor_scalar(
-                out=c8[:].rearrange("p g t -> p (g t)"), in0=c_bf[:].rearrange("p g t -> p (g t)"),
-                scalar1=0.125, scalar2=None, op0=ALU.mult,
+                out=out_factor[:].rearrange("p f t -> p (f t)"), in0=c_in[:].rearrange("p f t -> p (f t)"),
+                scalar1=32.0 / N_EX, scalar2=None, op0=ALU.mult,
             )
-            for half in range(2):
-                rows = slice(64 * half, 64 * half + 64)
-                nc.vector.tensor_copy(out=wm[rows, half, :], in_=wab[rows, :])
-
+            for e in range(2):
+                rows = slice(64 * e, 64 * e + 64)
+                nc.vector.tensor_copy(out=group_weight[rows, e, :], in_=loss_weight[rows, :])
 
         tiles = {}
 
-        def tr(i):
-            q, j = divmod(i, 4)
-            words = x[q][:, j, :].bitcast(F32)
-            t = bank(i % 2, [P, 2, 2, P], "tr")
-            for g in range(2):
+        def transpose_words(i):
+            s, j = divmod(i, 4)
+            words = x[s][:, j, :].bitcast(F32)
+            t = bank(i % 2, [P, F_GROUPS, 2, P], "words")
+            for f in range(F_GROUPS):
                 for u in range(2):
-                    nc.tensor.transpose(t[:, g, u, :], words[:, 256 * g + u : 256 * (g + 1) : 2], ident_f[:])
-            tiles["tr", i] = t
+                    nc.tensor.transpose(t[:, f, u, :], words[:, 256 * f + u : 256 * (f + 1) : 2], ident_f[:])
+            tiles["words", i] = t
 
-        def copy(i):
-            hq = work.tile([P, D], BF16, name="hq", tag="hq", bufs=3, align_bytes=64)
+        def copy_words(i):
+            ht = work.tile([P, D], BF16, name="ht", tag="ht", bufs=3, align_bytes=64)
             nc.scalar.copy(
-                out=hq[:].bitcast(F32).rearrange("p (g r u) -> p g r u", g=2, u=2),
-                in_=tiles["tr", i][:].rearrange("p g u r -> p g r u"),
+                out=ht[:].bitcast(F32).rearrange("p (f r u) -> p f r u", f=F_GROUPS, u=2),
+                in_=tiles["words", i][:].rearrange("p f u r -> p f r u"),
             )
-            tiles["hq", i] = hq
+            tiles["ht", i] = ht
 
-        def quant(i):
-            hc = work.tile([P, 256], U32, name="hc", tag="hc", bufs=3, align_bytes=64)
-            hs = work.tile([P, 256], U8, name="hs", tag="hs", bufs=3, align_bytes=64)
-            nc.vector.quantize_mx(out=hc[:].bitcast(FP8X4), scales=hs[:], in_=tiles["hq", i][:])
-            tiles["hc", i] = (hc, hs)
+        def quantize_h(i):
+            codes = work.tile([P, F_GROUPS * P], U32, name="h_codes", tag="h_codes", bufs=3, align_bytes=64)
+            scales = work.tile([P, F_GROUPS * P], U8, name="h_scales", tag="h_scales", bufs=3, align_bytes=64)
+            nc.vector.quantize_mx(out=codes[:].bitcast(FP8X4), scales=scales[:], in_=tiles["ht", i][:])
+            tiles["h", i] = (codes, scales)
 
-        def zmm(i):
-            hc, hs = tiles["hc", i]
+        def z_passes(i):
+            codes, scales = tiles["h", i]
             z = bank(2 + i % 4, [P, C], "z")
-            for g in range(2):
+            for f in range(F_GROUPS):
+                cols = slice(f * P, (f + 1) * P)
                 nc.tensor.matmul_mx(
                     out=z[:],
-                    lhsT=hc[:, g * P : (g + 1) * P].bitcast(FP8X4),
-                    lhsT_scale=hs[:, g * P : (g + 1) * P],
-                    rhs=ww[:, g, :].bitcast(FP4X4),
-                    rhs_scale=ws[:, g, :],
-                    start=(g == 0),
-                    stop=(g == 1),
+                    lhsT=codes[:, cols].bitcast(FP8X4),
+                    lhsT_scale=scales[:, cols],
+                    rhs=w_sb[:, f, :].bitcast(FP4X4),
+                    rhs_scale=w_sc[:, f, :],
+                    start=(f == 0),
+                    stop=(f == F_GROUPS - 1),
                 )
             tiles["z", i] = z
 
-        def bymm(i):
-            q, j = divmod(i, 4)
+        def by_product(i):
+            s, j = divmod(i, 4)
             t = bank(6 + i % 2, [P, C], "by")
-            nc.tensor.matmul(t[:], lhsT=dg[:, i, :], rhs=yt[q][:, j, :], start=True, stop=True)
+            nc.tensor.matmul(t[:], lhsT=diag_b[:, i, :], rhs=y_in[s][:, j, :], start=True, stop=True)
             tiles["by", i] = t
 
-        def absz(i):
-            az = work.tile([P, C], F32, name="az", tag="az", bufs=2)
-            nc.scalar.activation(out=az[:], in_=tiles["z", i][:], func=ACT.Abs, accum_out=abs_acc[:, i : i + 1])
-            tiles["az", i] = az
+        def abs_z(i):
+            t = work.tile([P, C], F32, name="az", tag="az", bufs=2)
+            nc.scalar.activation(out=t[:], in_=tiles["z", i][:], func=ACT.Abs, accum_out=abs_sum[:, i : i + 1])
+            tiles["az", i] = t
 
-        def sig(i):
-            s = work.tile([P, C], F32, name="s", tag="s", bufs=4)
-            nc.scalar.activation(out=s[:], in_=tiles["z", i][:], func=ACT.Sigmoid)
-            tiles["s", i] = s
+        def sigmoid_z(i):
+            t = work.tile([P, C], F32, name="sig", tag="sig", bufs=5)
+            nc.scalar.activation(out=t[:], in_=tiles["z", i][:], func=ACT.Sigmoid)
+            tiles["sig", i] = t
 
-        def sigaz(i):
-            u = work.tile([P, C], F32, name="u", tag="u", bufs=3)
-            nc.scalar.activation(out=u[:], in_=tiles["az", i][:], func=ACT.Sigmoid)
-            tiles["u", i] = u
+        def sigmoid_abs_z(i):
+            t = work.tile([P, C], F32, name="sig_abs", tag="sig_abs", bufs=3)
+            nc.scalar.activation(out=t[:], in_=tiles["az", i][:], func=ACT.Sigmoid)
+            tiles["sig_abs", i] = t
 
-        def yz(i):
-            q, j = divmod(i, 4)
-            junk = work.tile([P, C], BF16, name="junk", tag="junk", bufs=2)
-            nc.vector.scalar_tensor_tensor(
-                out=junk[:], in0=yt[q][:, j, :], scalar=0.5, in1=tiles["z", i][:],
-                op0=ALU.subtract, op1=ALU.mult, accum_out=yz_acc[:, i : i + 1],
-            )
-
-        def prod(i):
+        def product_of_sigmoids(i):
             nc.vector.tensor_reduce(
-                out=prods[:, i, :], in_=tiles["u", i][:].rearrange("p (s e) -> p s e", s=8), axis=AX.X, op=ALU.mult
+                out=products[:, i, :], in_=tiles["sig_abs", i][:].rearrange("p (n e) -> p n e", e=FACTORS),
+                axis=AX.X, op=ALU.mult,
             )
 
-        def bdelta(i):
-            q, j = divmod(i, 4)
+        def sum_of_yz(i):
+            s, j = divmod(i, 4)
+            t = work.tile([P, C], BF16, name="yz", tag="yz", bufs=2)
             nc.vector.scalar_tensor_tensor(
-                out=bd[q][:, j, :], in0=tiles["s", i][:], scalar=b_col[:, i : i + 1], in1=tiles["by", i][:],
+                out=t[:], in0=y_in[s][:, j, :], scalar=half[:], in1=tiles["z", i][:],
+                op0=ALU.subtract, op1=ALU.mult, accum_out=yz_sum[:, i : i + 1],
+            )
+
+        def make_residual(i):
+            s, j = divmod(i, 4)
+            nc.vector.scalar_tensor_tensor(
+                out=residual[s][:, j, :], in0=tiles["sig", i][:], scalar=b_col[:, i : i + 1], in1=tiles["by", i][:],
                 op0=ALU.mult, op1=ALU.subtract,
             )
 
-        xs = {}
-        wb = {}
+        wx = {}
+        wh = {}
 
-        def amult(i):
-            q, j = divmod(i, 4)
+        def multiply_by_a(i):
+            s, j = divmod(i, 4)
             if j == 0:
-                xs[q] = work.tile([P, 4, D], BF16, name="xs", tag="xs", bufs=3)
-                wb[q] = work.tile([P, 2, 4, P, 4], BF16, name="wb", tag="wb", bufs=3, align_bytes=64)
+                wx[s] = work.tile([P, 4, D], BF16, name="wx", tag="wx", bufs=3)
+                wh[s] = work.tile([P, F_GROUPS, 4, P, 4], BF16, name="wh", tag="wh", bufs=3, align_bytes=64)
             nc.vector.tensor_scalar(
-                out=xs[q][:, j, :], in0=x[q][:, j, :], scalar1=a_col[:, i : i + 1], scalar2=None, op0=ALU.mult
+                out=wx[s][:, j, :], in0=x[s][:, j, :], scalar1=a_col[:, i : i + 1], scalar2=None, op0=ALU.mult
             )
 
-        def inter(q, g, tp, eng, m0, mn):
-            copy_fn = nc.vector.tensor_copy if eng == "v" else nc.scalar.copy
+        def interleave(copy_fn, s, fg, m0, m_count):
             copy_fn(
-                out=wb[q][:, g, 2 * tp : 2 * tp + 2, m0 : m0 + mn, :].rearrange("p t m j -> p m t j"),
-                in_=xs[q][:, :, g * C : (g + 1) * C].rearrange("p j (m t) -> p m t j", t=4)[:, m0 : m0 + mn, 2 * tp : 2 * tp + 2],
+                out=wh[s][:, fg].rearrange("p t m j -> p m t j")[:, m0 : m0 + m_count],
+                in_=wx[s][:, :, fg * STRETCH : (fg + 1) * STRETCH]
+                .rearrange("p j (m t) -> p m t j", t=4)[:, m0 : m0 + m_count],
             )
 
-        def wquant(q, g):
-            cols = slice(g * C, (g + 1) * C)
+        def quantize_wh(s, fg):
+            cols = slice(fg * STRETCH, (fg + 1) * STRETCH)
             nc.vector.quantize_mx(
-                out=w_codes[q][:, cols].bitcast(FP8X4), scales=w_planes[q][:, cols],
-                in_=wb[q][:, g].rearrange("p t m j -> p (t m j)"),
+                out=wh_codes[s][:, cols].bitcast(FP8X4), scales=wh_scales[s][:, cols],
+                in_=wh[s][:, fg].rearrange("p t m j -> p (t m j)"),
             )
 
-        v_c = {}
-        s_c = {}
-
-        def at(table, step, f, *args):
-            table.setdefault(step, []).append(lambda: f(*args))
-
-        for i in range(TILES):
-            at(v_c, max(i, 2), amult, i)
-        for q in range(3):
-            for n in range(2):
-                at(v_c, 4 * q + 5 + n, inter, q, 0, n, "v", 0, P)
-            for n in range(4):
-                at(s_c, 4 * q + 4 + n, inter, q, 1, n // 2, "s", 64 * (n % 2), 64)
-            if q < 2:
-                at(v_c, 4 * q + 8, wquant, q, 0)
-                at(v_c, 4 * q + 10, wquant, q, 1)
-        for n in range(2):
-            at(s_c, 16, inter, 3, 1, 0, "s", 64 * n, 64)
-
-        for n in range(WARM1):
-            nc.tensor.matmul(bank(7, [P, P], "warm1")[:], lhsT=ident_b[:], rhs=ident_b[:], start=True, stop=True)
-        tr(0)
-        tr(1)
-        for k in range(TILES + 2):
-            if 2 <= k < TILES + 1:
-                absz(k - 2)
-                sig(k - 2)
+        transpose_words(0)
+        transpose_words(1)
+        for k in range(TILES + LAG):
+            seen = k - LAG
+            done = seen - 1
+            last = seen == TILES - 1
+            if seen >= 0:
+                abs_z(seen)
+                if last:
+                    sigmoid_abs_z(seen)
+                sigmoid_z(seen)
             if k < TILES:
-                copy(k)
-            if 2 <= k < TILES + 1:
-                sigaz(k - 2)
-            if k == TILES + 1:
-                absz(k - 2)
-                sigaz(k - 2)
-                sig(k - 2)
-            if 1 <= k < TILES + 1:
-                quant(k - 1)
-                zmm(k - 1)
-            if 3 <= k:
-                prod(k - 3)
+                copy_words(k)
+            if seen >= 0 and not last:
+                sigmoid_abs_z(seen)
+            if 1 <= k <= TILES:
+                quantize_h(k - 1)
+                z_passes(k - 1)
+            if done >= 0:
+                product_of_sigmoids(done)
             if k + 2 < TILES:
-                tr(k + 2)
-            if 2 <= k:
-                bymm(k - 2)
-            for f in s_c.get(k, []):
-                f()
-            if 3 <= k:
-                yz(k - 3)
-            for f in v_c.get(k, []):
-                f()
+                transpose_words(k + 2)
+            if seen >= 0:
+                by_product(seen)
+            s, quarter = divmod(k - 4, 4)
+            if 0 <= s < SPANS - 1:
+                interleave(nc.scalar.copy, s, 1, 32 * quarter, 32)
+            if done >= 0:
+                sum_of_yz(done)
+            if 2 <= k < TILES:
+                for i in range(0 if k == 2 else k, k + 1):
+                    multiply_by_a(i)
+            for fg, behind in ((0, 8), (1, 10)):
+                s, rest = divmod(k - behind, 4)
+                if rest == 0 and 0 <= s < 2:
+                    quantize_wh(s, fg)
+            s, part = divmod(k - 5, 4)
+            if 0 <= s < SPANS - 1 and part < 2:
+                interleave(nc.vector.tensor_copy, s, 0, 64 * part, 64)
             if k == 1:
-                for i in range(TILES):
-                    diag_b(i)
+                diagonals_of_b()
             if k == 5:
-                weights()
-            if 3 <= k:
-                bdelta(k - 3)
-        for f in v_c.get(TILES + 2, []):
-            f()
+                loss_weights()
+            if done >= 0:
+                make_residual(done)
 
-        prod(TILES - 1)
-        yz(TILES - 1)
-        lnp = keep.tile([P, TILES, 8], F32, name="lnp")
-        nc.scalar.activation(out=lnp[:], in_=prods[:], func=ACT.Ln)
-        wquant(2, 0)
-        wquant(2, 1)
-        lin = keep.tile([P, TILES], F32, name="lin")
-        lnu = keep.tile([P, TILES], F32, name="lnu")
-        nc.vector.tensor_reduce(out=lnu[:], in_=lnp[:], axis=AX.X, op=ALU.add)
+        end = TILES - 1
+        product_of_sigmoids(end)
+        sum_of_yz(end)
+        logs = keep.tile([P, TILES, C // FACTORS], F32, name="logs")
+        nc.scalar.activation(out=logs[:], in_=products[:], func=ACT.Ln)
+        interleave(nc.scalar.copy, SPANS - 1, 1, 0, LAST_SHARE)
+        quantize_wh(SPANS - 2, 0)
+        quantize_wh(SPANS - 2, 1)
+        log_sum = keep.tile([P, TILES], F32, name="log_sum")
+        nc.vector.tensor_reduce(out=log_sum[:], in_=logs[:], axis=AX.X, op=ALU.add)
+        linear = keep.tile([P, TILES], F32, name="linear")
         nc.vector.scalar_tensor_tensor(
-            out=lin[:], in0=abs_acc[:], scalar=-0.5, in1=yz_acc[:], op0=ALU.mult, op1=ALU.add
+            out=linear[:], in0=abs_sum[:], scalar=-0.5, in1=yz_sum[:], op0=ALU.mult, op1=ALU.add
         )
-        rhs1 = keep.tile([P, 2, TILES], F32, name="rhs1")
-        rhs2 = keep.tile([P, 2, TILES], F32, name="rhs2")
+        weighted_log = keep.tile([P, 2, TILES], F32, name="weighted_log")
+        weighted_lin = keep.tile([P, 2, TILES], F32, name="weighted_lin")
         nc.vector.tensor_tensor(
-            out=rhs2[:], in0=lnu[:].unsqueeze(1).to_broadcast([P, 2, TILES]), in1=wm[:], op=ALU.mult
+            out=weighted_log[:], in0=log_sum[:].unsqueeze(1).to_broadcast([P, 2, TILES]), in1=group_weight[:],
+            op=ALU.mult,
         )
         nc.vector.tensor_tensor(
-            out=rhs1[:], in0=lin[:].unsqueeze(1).to_broadcast([P, 2, TILES]), in1=wm[:], op=ALU.mult
+            out=weighted_lin[:], in0=linear[:].unsqueeze(1).to_broadcast([P, 2, TILES]), in1=group_weight[:],
+            op=ALU.mult,
         )
-        rhs1_first = rhs1[0:1].rearrange("o e (q j) -> o e q j", j=4)[:, :, :, 0]
+        first = weighted_lin[0:1].rearrange("o e (s j) -> o e s j", j=4)[:, :, :, 0]
         nc.vector.scalar_tensor_tensor(
-            out=rhs1_first, in0=adj_bf[:].rearrange("o (q e) -> o e q", e=2), scalar=-0.125, in1=rhs1_first,
+            out=first, in0=adj_in[:].rearrange("o (s e) -> o e s", e=2), scalar=-ETA, in1=first,
             op0=ALU.mult, op1=ALU.add,
         )
-        nv_bank = bank(0, [P, 2 * TILES], "nv")
-        nc.tensor.matmul(nv_bank[:], lhsT=ones[:], rhs=rhs2[:].rearrange("p e i -> p (e i)"), start=True, stop=False)
-        nc.tensor.matmul(nv_bank[:], lhsT=ones[:], rhs=rhs1[:].rearrange("p e i -> p (e i)"), start=False, stop=True)
-        inter(3, 0, 0, "v", 0, P)
-        nv = keep.tile([P, N_GROUPS], F32, name="nv")
-        nc.vector.tensor_reduce(
-            out=nv[:], in_=nv_bank[:].rearrange("p (g j) -> p g j", j=4), axis=AX.X, op=ALU.add
+        sums = bank(0, [P, 2 * TILES], "sums")
+        nc.tensor.matmul(
+            sums[:], lhsT=ones[:], rhs=weighted_log[:].rearrange("p e i -> p (e i)"), start=True, stop=False
         )
-        nmax = keep.tile([P, 1], F32, name="nmax")
-        nc.vector.tensor_reduce(out=nmax[:], in_=nv[:], axis=AX.X, op=ALU.min)
-        e = keep.tile([P, N_GROUPS], F32, name="e")
-        esum = keep.tile([P, 1], F32, name="esum")
-        nc.scalar.activation(out=e[:], in_=nv[:], func=ACT.Exp, scale=-1.0, bias=nmax[:], accum_out=esum[:])
-        bdelta(TILES - 1)
-        rinv = keep.tile([P, 1], F32, name="rinv")
-        nc.vector.reciprocal(out=rinv[:], in_=esum[:])
-        qv = keep.tile([P, PASSES], F32, name="qv")
-        for half in range(2):
-            rows = slice(64 * half, 64 * half + 64)
+        nc.tensor.matmul(
+            sums[:], lhsT=ones[:], rhs=weighted_lin[:].rearrange("p e i -> p (e i)"), start=False, stop=True
+        )
+        interleave(nc.vector.tensor_copy, SPANS - 1, 0, 0, 64)
+        neg_v = keep.tile([P, N_GROUPS], F32, name="neg_v")
+        nc.vector.tensor_reduce(
+            out=neg_v[:], in_=sums[:].rearrange("p (g j) -> p g j", j=4), axis=AX.X, op=ALU.add
+        )
+        neg_max = keep.tile([P, 1], F32, name="neg_max")
+        nc.vector.tensor_reduce(out=neg_max[:], in_=neg_v[:], axis=AX.X, op=ALU.min)
+        exps = keep.tile([P, N_GROUPS], F32, name="exps")
+        exp_sum = keep.tile([P, 1], F32, name="exp_sum")
+        nc.scalar.activation(
+            out=exps[:], in_=neg_v[:], func=ACT.Exp, scale=-1.0, bias=neg_max[:], accum_out=exp_sum[:]
+        )
+        make_residual(end)
+        inverse = keep.tile([P, 1], F32, name="inverse")
+        nc.vector.reciprocal(out=inverse[:], in_=exp_sum[:])
+        soft = keep.tile([P, SPANS], F32, name="soft")
+        for e in range(2):
+            rows = slice(64 * e, 64 * e + 64)
             nc.vector.tensor_scalar(
-                out=qv[rows, :], in0=e[rows, 4 * half : 4 * half + 4], scalar1=rinv[rows, :], scalar2=None, op0=ALU.mult
+                out=soft[rows, :], in0=exps[rows, SPANS * e : SPANS * (e + 1)], scalar1=inverse[rows, :],
+                scalar2=None, op0=ALU.mult,
             )
 
-        for n in range(WARM2):
-            hc, hs = tiles["hc", TILES - 1]
-            nc.tensor.matmul_mx(
-                out=bank(7, [P, C], "warm2")[:], lhsT=hc[:, 0:P].bitcast(FP8X4), lhsT_scale=hs[:, 0:P],
-                rhs=ww[:, 0, :].bitcast(FP4X4), rhs_scale=ws[:, 0, :], start=True, stop=True,
-            )
+        deltas = {}
 
-        dl = {}
-
-        def delta(q, ha):
-            t = work.tile([P, KH, 4], BF16, name="dl", tag="dl", bufs=3, align_bytes=64)
-            src = bd[q][:, :, ha * KH : (ha + 1) * KH].rearrange("p j k -> p k j")
+        def make_delta(s, kh):
+            t = work.tile([P, HALF_C, 4], BF16, name="delta", tag="delta", bufs=3, align_bytes=64)
+            src = residual[s][:, :, kh * HALF_C : (kh + 1) * HALF_C].rearrange("p j k -> p k j")
             nc.vector.tensor_scalar(
-                out=t[:, :V_COLS, :], in0=src[:, :V_COLS, :], scalar1=qv[:, q : q + 1], scalar2=None, op0=ALU.mult
+                out=t[:, :V_COLS, :], in0=src[:, :V_COLS, :], scalar1=soft[:, s : s + 1], scalar2=None, op0=ALU.mult
             )
-            nc.scalar.activation(out=t[:, V_COLS:, :], in_=src[:, V_COLS:, :], func=ACT.Copy, scale=qv[:, q : q + 1])
-            dl[q, ha] = t
+            nc.scalar.activation(
+                out=t[:, V_COLS:, :], in_=src[:, V_COLS:, :], func=ACT.Copy, scale=soft[:, s : s + 1]
+            )
+            deltas[s, kh] = t
 
-        def dquant(q, ha):
-            cols = slice(ha * KH, (ha + 1) * KH)
+        def quantize_delta(s, kh):
+            cols = slice(kh * HALF_C, (kh + 1) * HALF_C)
             nc.vector.quantize_mx(
-                out=d_codes[q][:, cols].bitcast(FP8X4), scales=d_planes[q][:, cols],
-                in_=dl[q, ha][:].rearrange("p k j -> p (k j)"),
+                out=dl_codes[s][:, cols].bitcast(FP8X4), scales=dl_scales[s][:, cols],
+                in_=deltas[s, kh][:].rearrange("p k j -> p (k j)"),
             )
 
-        def gmm(out, q, g, t, ha):
-            sl = slice(g * C + t * P, g * C + (t + 1) * P)
-            cols = slice(ha * KH, (ha + 1) * KH)
+        for kh in range(2):
+            make_delta(0, kh)
+            for s in range(1, SPANS):
+                make_delta(s, kh)
+                quantize_delta(s - 1, kh)
+            if kh == 0:
+                interleave(nc.vector.tensor_copy, SPANS - 1, 0, 64, 64)
+                interleave(nc.vector.tensor_copy, SPANS - 1, 1, LAST_SHARE, P - LAST_SHARE)
+                quantize_wh(SPANS - 1, 0)
+                quantize_wh(SPANS - 1, 1)
+            quantize_delta(SPANS - 1, kh)
+
+        def grad_pass(out, s, fg, t, kh):
+            feats = slice(fg * STRETCH + t * P, fg * STRETCH + (t + 1) * P)
+            cols = slice(kh * HALF_C, (kh + 1) * HALF_C)
             nc.tensor.matmul_mx(
                 out=out,
-                lhsT=w_codes[q][:, sl].bitcast(FP8X4),
-                lhsT_scale=w_planes[q][:, sl],
-                rhs=d_codes[q][:, cols].bitcast(FP8X4),
-                rhs_scale=d_planes[q][:, cols],
-                start=(q == 0),
-                stop=(q == PASSES - 1),
+                lhsT=wh_codes[s][:, feats].bitcast(FP8X4),
+                lhsT_scale=wh_scales[s][:, feats],
+                rhs=dl_codes[s][:, cols].bitcast(FP8X4),
+                rhs_scale=dl_scales[s][:, cols],
+                start=(s == 0),
+                stop=(s == SPANS - 1),
             )
 
-        delta(0, 0)
-        delta(1, 0)
-        dquant(0, 0)
-        delta(2, 0)
-        dquant(1, 0)
-        delta(3, 0)
-        dquant(2, 0)
-        inter(3, 0, 1, "v", 0, P)
-        inter(3, 1, 1, "v", 0, P)
-        wquant(3, 0)
-        wquant(3, 1)
-        dquant(3, 0)
-        delta(0, 1)
-        delta(1, 1)
-        dquant(0, 1)
-        delta(2, 1)
-        dquant(1, 1)
-        delta(3, 1)
-        dquant(2, 1)
-        dquant(3, 1)
+        out_rows = out_0.rearrange("(f p t) k -> f p t k", p=P, t=4)
+        out_words = out_1.rearrange("f p m t -> f p (m t)")
+        out_sc = keep.tile([P, F_GROUPS, C], U8, name="out_sc", align_bytes=64)
 
-        out_rows = out_0.rearrange("(g p t) k -> g p t k", p=P, t=4)
-        osc = keep.tile([P, 2, C], U8, name="osc", align_bytes=64)
-
-        def scales_out():
-            for r in range(4):
-                eng = nc.sync if r % 2 else nc.scalar
-                eng.dma_start(
-                    out=out_2[:, 4 * r : 4 * r + 4, :].rearrange("g r m -> r g m").bitcast(I32),
-                    in_=osc[32 * r : 32 * r + 4, :, :].bitcast(I32),
-                )
-
-        def finish(g, ha, banks, stores):
-            cols = slice(ha * KH, (ha + 1) * KH)
-            of = work.tile([P, 4, KH], F32, name="of", tag="of", bufs=4)
+        def finish(fg, kh, banks):
+            cols = slice(kh * HALF_C, (kh + 1) * HALF_C)
+            res = work.tile([P, 4, HALF_C], F32, name="res", tag="res", bufs=4)
             for t in range(4):
-                nc.scalar.activation(out=of[:, t, :], in_=banks[t][:], func=ACT.Copy, scale=c8[:, g, t : t + 1])
-            for t in range(0, 4, 4 // stores):
-                ts = slice(t, t + 4 // stores)
-                nc.sync.dma_start(out=out_rows[g][:, ts, cols], in_=of[:, ts, :])
-            ob = work.tile([P, KH, 4], BF16, name="ob", tag="ob", bufs=2, align_bytes=64)
-            oc = keep.tile([P, KH], U32, name="oc_%d_%d" % (g, ha), align_bytes=64)
-            nc.vector.tensor_copy(out=ob[:], in_=of[:].rearrange("p t k -> p k t"))
+                nc.scalar.activation(
+                    out=res[:, t, :], in_=banks[t][:], func=ACT.Copy, scale=out_factor[:, fg, t : t + 1]
+                )
+            nc.sync.dma_start(out=out_rows[fg][:, :, cols], in_=res[:])
+            packed = work.tile([P, HALF_C, 4], BF16, name="packed", tag="packed", bufs=2, align_bytes=64)
+            codes = keep.tile([P, HALF_C], U32, name="out_codes_%d_%d" % (fg, kh), align_bytes=64)
+            nc.vector.tensor_copy(out=packed[:], in_=res[:].rearrange("p t k -> p k t"))
             nc.vector.quantize_mx(
-                out=oc[:].bitcast(FP8X4), scales=osc[:, g, cols], in_=ob[:].rearrange("p k t -> p (k t)")
+                out=codes[:].bitcast(FP8X4), scales=out_sc[:, fg, cols], in_=packed[:].rearrange("p k t -> p (k t)")
             )
             nc.sync.dma_start(
-                out=out_1[g].rearrange("p m t -> p (m t)")[:, 4 * ha * KH : 4 * (ha + 1) * KH].bitcast(I32),
-                in_=oc[:].bitcast(I32),
+                out=out_words[fg][:, 4 * kh * HALF_C : 4 * (kh + 1) * HALF_C].bitcast(I32), in_=codes[:].bitcast(I32)
             )
 
-        ba = [bank(t, [P, KH], "ga") for t in range(8)]
-        for q in range(PASSES):
-            for t in range(8):
-                gmm(ba[t][:], q, t // 4, t % 4, 0)
-        finish(0, 0, ba[:4], 1)
-        finish(1, 0, ba[4:], 1)
-        bb = [bank(t, [P, KH], "gb") for t in range(4)]
-        for q in range(PASSES):
+        grad = [bank(n, [P, HALF_C], "grad_a") for n in range(8)]
+        for s in range(SPANS):
+            for n in range(8):
+                grad_pass(grad[n][:], s, n // 4, n % 4, 0)
+        finish(0, 0, grad[:4])
+        finish(1, 0, grad[4:])
+        grad = [bank(n, [P, HALF_C], "grad_b") for n in range(4)]
+        for s in range(SPANS):
             for t in range(4):
-                gmm(bb[t][:], q, 0, t, 1)
-        finish(0, 1, bb, 1)
-        bc = [bank(4 + t, [P, KH], "gb") for t in range(4)]
+                grad_pass(grad[t][:], s, 0, t, 1)
+        finish(0, 1, grad)
+        grad = [bank(4 + n, [P, HALF_C], "grad_b") for n in range(4)]
         for t in range(4):
-            for q in range(PASSES):
-                gmm(bc[t][:], q, 1, t, 1)
-        finish(1, 1, bc, 1)
-        scales_out()
+            for s in range(SPANS):
+                grad_pass(grad[t][:], s, 1, t, 1)
+        finish(1, 1, grad)
+        for quad in range(4):
+            queue = nc.sync if quad % 2 else nc.scalar
+            queue.dma_start(
+                out=out_2[:, 4 * quad : 4 * quad + 4, :].rearrange("f r m -> r f m").bitcast(I32),
+                in_=out_sc[32 * quad : 32 * quad + 4, :, :].bitcast(I32),
+            )

from contextlib import ExitStack

import concourse.mybir as mybir
from concourse.masks import make_identity

F32 = mybir.dt.float32
BF16 = mybir.dt.bfloat16
U32 = mybir.dt.uint32
I32 = mybir.dt.int32
U8 = mybir.dt.uint8
FP8X4 = mybir.dt.float8_e4m3fn_x4
FP4X4 = mybir.dt.float4_e2m1fn_x4
ACT = mybir.ActivationFunctionType
ALU = mybir.AluOpType
AX = mybir.AxisListType

N_GROUPS, N_EX, D, C = 8, 256, 1024, 512
ETA = 0.125
P = 128
PACK = 4
STRETCH = P * PACK
TOKENS = N_GROUPS * N_EX
SPANS = TOKENS // STRETCH
TILES = TOKENS // P
F_GROUPS = D // STRETCH
HALF_C = C // 2
FACTORS = 64

LAG = 3
V_COLS = 128
LAST_SHARE = 64

FLOPS = 2 * (2 * TOKENS * D * C)


def tile_groupdrologsumexppreconditionedgradient_x2_kernel(
    tc, h, w_words, w_scales, y, a, b, adj, c, out_0, out_1, out_2
):
    nc = tc.nc
    with ExitStack() as ctx:
        keep = ctx.enter_context(tc.tile_pool(name="keep", bufs=1))
        work = ctx.enter_context(tc.tile_pool(name="work", bufs=3))
        psum = ctx.enter_context(tc.psum_pool(name="psum", bufs=1))
        ctx.enter_context(tc.manual_schedule())

        def bank(index, shape, what):
            return psum.tile(shape, F32, name="%s_%d" % (what, index), tag="bank%d" % index, bufs=1)

        x = [keep.tile([P, 4, D], BF16, name="x%d" % s) for s in range(SPANS)]
        y_in = [keep.tile([P, 4, C], BF16, name="y%d" % s) for s in range(SPANS)]
        residual = [keep.tile([P, 4, C], F32, name="residual%d" % s) for s in range(SPANS)]
        wh_codes = [keep.tile([P, D], U32, name="wh_codes%d" % s, align_bytes=64) for s in range(SPANS)]
        wh_scales = [keep.tile([P, D], U8, name="wh_scales%d" % s, align_bytes=64) for s in range(SPANS)]
        dl_codes = [keep.tile([P, C], U32, name="dl_codes%d" % s, align_bytes=64) for s in range(SPANS)]
        dl_scales = [keep.tile([P, C], U8, name="dl_scales%d" % s, align_bytes=64) for s in range(SPANS)]
        w_sb = keep.tile([P, F_GROUPS, 2 * C], U8, name="w_sb", align_bytes=64)
        w_sc = keep.tile([P, F_GROUPS, C], U8, name="w_sc", align_bytes=64)
        a_in = keep.tile([P, SPANS, 4], BF16, name="a_in")
        b_in = keep.tile([P, SPANS, 4], BF16, name="b_in")
        c_in = keep.tile([P, F_GROUPS, 4], BF16, name="c_in")
        adj_in = keep.tile([1, N_GROUPS], BF16, name="adj_in")
        out_factor = keep.tile([P, F_GROUPS, 4], F32, name="out_factor")
        loss_weight = keep.tile([P, TILES], F32, name="loss_weight")
        group_weight = keep.tile([P, 2, TILES], F32, name="group_weight")
        ones = keep.tile([P, P], F32, name="ones")
        half = keep.tile([P, 1], F32, name="half")
        ident_f = keep.tile([P, P], F32, name="ident_f")
        ident_b = keep.tile([P, P], BF16, name="ident_b")
        diag_b = keep.tile([P, TILES, P], BF16, name="diag_b")
        abs_sum = keep.tile([P, TILES], F32, name="abs_sum")
        yz_sum = keep.tile([P, TILES], F32, name="yz_sum")
        products = keep.tile([P, TILES, C // FACTORS], F32, name="products")

        h_rows = h.rearrange("g n d -> (g n) d").rearrange("(s p j) d -> s p j d", p=P, j=4)
        y_rows = y.rearrange("g n k -> (g n) k").rearrange("(s p j) k -> s p j k", p=P, j=4)
        nc.vector.memset(w_sc[:].rearrange("p g n -> p (g n)").bitcast(I32), 0)
        make_identity(nc, ident_f[:])
        nc.sync.dma_start(out=x[0][:, 0, :], in_=h_rows[0][:, 0, :])
        nc.sync.dma_start(out=x[0][:, 1, :], in_=h_rows[0][:, 1, :])
        nc.sync.dma_start(out=w_sb[:].bitcast(I32), in_=w_words.rearrange("g p n -> p g n").bitcast(I32))
        nc.sync.dma_start(out=x[0][:, 2, :], in_=h_rows[0][:, 2, :])
        for quad in range(4):
            nc.scalar.dma_start(
                out=w_sc[32 * quad : 32 * quad + 4, :, :].bitcast(I32),
                in_=w_scales[:, 4 * quad : 4 * quad + 4, :].rearrange("g r n -> r g n").bitcast(I32),
            )
        nc.sync.dma_start(out=x[0][:, 3, :], in_=h_rows[0][:, 3, :])
        nc.sync.dma_start(out=b_in[:], in_=b.rearrange("g n -> (g n)").rearrange("(s p j) -> p s j", p=P, j=4))
        nc.sync.dma_start(out=y_in[0][:], in_=y_rows[0])
        nc.sync.dma_start(out=a_in[:], in_=a.rearrange("g n -> (g n)").rearrange("(s p j) -> p s j", p=P, j=4))
        nc.gpsimd.dma_start(out=adj_in[:], in_=adj.rearrange("(o g) -> o g", o=1))
        nc.gpsimd.dma_start(out=c_in[:], in_=c.rearrange("(f p t) -> p f t", p=P, t=4))
        for s in range(1, SPANS):
            nc.sync.dma_start(out=x[s][:, 0:2, :], in_=h_rows[s][:, 0:2, :])
            nc.sync.dma_start(out=x[s][:, 2:4, :], in_=h_rows[s][:, 2:4, :])
            nc.sync.dma_start(out=y_in[s][:], in_=y_rows[s])

        a_col = a_in[:].rearrange("p s j -> p (s j)")
        b_col = b_in[:].rearrange("p s j -> p (s j)")
        nc.vector.tensor_copy(out=ident_b[:], in_=ident_f[:])
        nc.vector.memset(ones[:], 1.0)
        nc.vector.memset(half[:], 0.0)
        nc.scalar.activation(out=half[:], in_=half[:], func=ACT.Sigmoid)
        nc.vector.memset(group_weight[:], 0.0)

        def diagonals_of_b():
            for i in range(TILES):
                nc.vector.tensor_scalar(
                    out=diag_b[:, i, :], in0=ident_b[:], scalar1=b_col[:, i : i + 1], scalar2=None, op0=ALU.mult
                )

        def loss_weights():
            nc.vector.scalar_tensor_tensor(
                out=loss_weight[:], in0=a_col, scalar=ETA / N_EX, in1=b_col, op0=ALU.mult, op1=ALU.mult
            )
            nc.vector.tensor_scalar(
                out=out_factor[:].rearrange("p f t -> p (f t)"), in0=c_in[:].rearrange("p f t -> p (f t)"),
                scalar1=32.0 / N_EX, scalar2=None, op0=ALU.mult,
            )
            for e in range(2):
                rows = slice(64 * e, 64 * e + 64)
                nc.vector.tensor_copy(out=group_weight[rows, e, :], in_=loss_weight[rows, :])

        tiles = {}

        def transpose_words(i):
            s, j = divmod(i, 4)
            words = x[s][:, j, :].bitcast(F32)
            t = bank(i % 2, [P, F_GROUPS, 2, P], "words")
            for f in range(F_GROUPS):
                for u in range(2):
                    nc.tensor.transpose(t[:, f, u, :], words[:, 256 * f + u : 256 * (f + 1) : 2], ident_f[:])
            tiles["words", i] = t

        def copy_words(i):
            ht = work.tile([P, D], BF16, name="ht", tag="ht", bufs=3, align_bytes=64)
            nc.scalar.copy(
                out=ht[:].bitcast(F32).rearrange("p (f r u) -> p f r u", f=F_GROUPS, u=2),
                in_=tiles["words", i][:].rearrange("p f u r -> p f r u"),
            )
            tiles["ht", i] = ht

        def quantize_h(i):
            codes = work.tile([P, F_GROUPS * P], U32, name="h_codes", tag="h_codes", bufs=3, align_bytes=64)
            scales = work.tile([P, F_GROUPS * P], U8, name="h_scales", tag="h_scales", bufs=3, align_bytes=64)
            nc.vector.quantize_mx(out=codes[:].bitcast(FP8X4), scales=scales[:], in_=tiles["ht", i][:])
            tiles["h", i] = (codes, scales)

        def z_passes(i):
            codes, scales = tiles["h", i]
            z = bank(2 + i % 4, [P, C], "z")
            for f in range(F_GROUPS):
                cols = slice(f * P, (f + 1) * P)
                nc.tensor.matmul_mx(
                    out=z[:],
                    lhsT=codes[:, cols].bitcast(FP8X4),
                    lhsT_scale=scales[:, cols],
                    rhs=w_sb[:, f, :].bitcast(FP4X4),
                    rhs_scale=w_sc[:, f, :],
                    start=(f == 0),
                    stop=(f == F_GROUPS - 1),
                )
            tiles["z", i] = z

        def by_product(i):
            s, j = divmod(i, 4)
            t = bank(6 + i % 2, [P, C], "by")
            nc.tensor.matmul(t[:], lhsT=diag_b[:, i, :], rhs=y_in[s][:, j, :], start=True, stop=True)
            tiles["by", i] = t

        def abs_z(i):
            t = work.tile([P, C], F32, name="az", tag="az", bufs=2)
            nc.scalar.activation(out=t[:], in_=tiles["z", i][:], func=ACT.Abs, accum_out=abs_sum[:, i : i + 1])
            tiles["az", i] = t

        def sigmoid_z(i):
            t = work.tile([P, C], F32, name="sig", tag="sig", bufs=5)
            nc.scalar.activation(out=t[:], in_=tiles["z", i][:], func=ACT.Sigmoid)
            tiles["sig", i] = t

        def sigmoid_abs_z(i):
            t = work.tile([P, C], F32, name="sig_abs", tag="sig_abs", bufs=3)
            nc.scalar.activation(out=t[:], in_=tiles["az", i][:], func=ACT.Sigmoid)
            tiles["sig_abs", i] = t

        def product_of_sigmoids(i):
            nc.vector.tensor_reduce(
                out=products[:, i, :], in_=tiles["sig_abs", i][:].rearrange("p (n e) -> p n e", e=FACTORS),
                axis=AX.X, op=ALU.mult,
            )

        def sum_of_yz(i):
            s, j = divmod(i, 4)
            t = work.tile([P, C], BF16, name="yz", tag="yz", bufs=2)
            nc.vector.scalar_tensor_tensor(
                out=t[:], in0=y_in[s][:, j, :], scalar=half[:], in1=tiles["z", i][:],
                op0=ALU.subtract, op1=ALU.mult, accum_out=yz_sum[:, i : i + 1],
            )

        def make_residual(i):
            s, j = divmod(i, 4)
            nc.vector.scalar_tensor_tensor(
                out=residual[s][:, j, :], in0=tiles["sig", i][:], scalar=b_col[:, i : i + 1], in1=tiles["by", i][:],
                op0=ALU.mult, op1=ALU.subtract,
            )

        wx = {}
        wh = {}

        def multiply_by_a(i):
            s, j = divmod(i, 4)
            if j == 0:
                wx[s] = work.tile([P, 4, D], BF16, name="wx", tag="wx", bufs=3)
                wh[s] = work.tile([P, F_GROUPS, 4, P, 4], BF16, name="wh", tag="wh", bufs=3, align_bytes=64)
            nc.vector.tensor_scalar(
                out=wx[s][:, j, :], in0=x[s][:, j, :], scalar1=a_col[:, i : i + 1], scalar2=None, op0=ALU.mult
            )

        def interleave(copy_fn, s, fg, m0, m_count):
            copy_fn(
                out=wh[s][:, fg].rearrange("p t m j -> p m t j")[:, m0 : m0 + m_count],
                in_=wx[s][:, :, fg * STRETCH : (fg + 1) * STRETCH]
                .rearrange("p j (m t) -> p m t j", t=4)[:, m0 : m0 + m_count],
            )

        def quantize_wh(s, fg):
            cols = slice(fg * STRETCH, (fg + 1) * STRETCH)
            nc.vector.quantize_mx(
                out=wh_codes[s][:, cols].bitcast(FP8X4), scales=wh_scales[s][:, cols],
                in_=wh[s][:, fg].rearrange("p t m j -> p (t m j)"),
            )

        transpose_words(0)
        transpose_words(1)
        for k in range(TILES + LAG):
            seen = k - LAG
            done = seen - 1
            last = seen == TILES - 1
            if seen >= 0:
                abs_z(seen)
                if last:
                    sigmoid_abs_z(seen)
                sigmoid_z(seen)
            if k < TILES:
                copy_words(k)
            if seen >= 0 and not last:
                sigmoid_abs_z(seen)
            if 1 <= k <= TILES:
                quantize_h(k - 1)
                z_passes(k - 1)
            if done >= 0:
                product_of_sigmoids(done)
            if k + 2 < TILES:
                transpose_words(k + 2)
            if seen >= 0:
                by_product(seen)
            s, quarter = divmod(k - 4, 4)
            if 0 <= s < SPANS - 1:
                interleave(nc.scalar.copy, s, 1, 32 * quarter, 32)
            if done >= 0:
                sum_of_yz(done)
            if 2 <= k < TILES:
                for i in range(0 if k == 2 else k, k + 1):
                    multiply_by_a(i)
            for fg, behind in ((0, 8), (1, 10)):
                s, rest = divmod(k - behind, 4)
                if rest == 0 and 0 <= s < 2:
                    quantize_wh(s, fg)
            s, part = divmod(k - 5, 4)
            if 0 <= s < SPANS - 1 and part < 2:
                interleave(nc.vector.tensor_copy, s, 0, 64 * part, 64)
            if k == 1:
                diagonals_of_b()
            if k == 5:
                loss_weights()
            if done >= 0:
                make_residual(done)

        end = TILES - 1
        product_of_sigmoids(end)
        sum_of_yz(end)
        logs = keep.tile([P, TILES, C // FACTORS], F32, name="logs")
        nc.scalar.activation(out=logs[:], in_=products[:], func=ACT.Ln)
        interleave(nc.scalar.copy, SPANS - 1, 1, 0, LAST_SHARE)
        quantize_wh(SPANS - 2, 0)
        quantize_wh(SPANS - 2, 1)
        log_sum = keep.tile([P, TILES], F32, name="log_sum")
        nc.vector.tensor_reduce(out=log_sum[:], in_=logs[:], axis=AX.X, op=ALU.add)
        linear = keep.tile([P, TILES], F32, name="linear")
        nc.vector.scalar_tensor_tensor(
            out=linear[:], in0=abs_sum[:], scalar=-0.5, in1=yz_sum[:], op0=ALU.mult, op1=ALU.add
        )
        weighted_log = keep.tile([P, 2, TILES], F32, name="weighted_log")
        weighted_lin = keep.tile([P, 2, TILES], F32, name="weighted_lin")
        nc.vector.tensor_tensor(
            out=weighted_log[:], in0=log_sum[:].unsqueeze(1).to_broadcast([P, 2, TILES]), in1=group_weight[:],
            op=ALU.mult,
        )
        nc.vector.tensor_tensor(
            out=weighted_lin[:], in0=linear[:].unsqueeze(1).to_broadcast([P, 2, TILES]), in1=group_weight[:],
            op=ALU.mult,
        )
        first = weighted_lin[0:1].rearrange("o e (s j) -> o e s j", j=4)[:, :, :, 0]
        nc.vector.scalar_tensor_tensor(
            out=first, in0=adj_in[:].rearrange("o (s e) -> o e s", e=2), scalar=-ETA, in1=first,
            op0=ALU.mult, op1=ALU.add,
        )
        sums = bank(0, [P, 2 * TILES], "sums")
        nc.tensor.matmul(
            sums[:], lhsT=ones[:], rhs=weighted_log[:].rearrange("p e i -> p (e i)"), start=True, stop=False
        )
        nc.tensor.matmul(
            sums[:], lhsT=ones[:], rhs=weighted_lin[:].rearrange("p e i -> p (e i)"), start=False, stop=True
        )
        interleave(nc.vector.tensor_copy, SPANS - 1, 0, 0, 64)
        neg_v = keep.tile([P, N_GROUPS], F32, name="neg_v")
        nc.vector.tensor_reduce(
            out=neg_v[:], in_=sums[:].rearrange("p (g j) -> p g j", j=4), axis=AX.X, op=ALU.add
        )
        neg_max = keep.tile([P, 1], F32, name="neg_max")
        nc.vector.tensor_reduce(out=neg_max[:], in_=neg_v[:], axis=AX.X, op=ALU.min)
        exps = keep.tile([P, N_GROUPS], F32, name="exps")
        exp_sum = keep.tile([P, 1], F32, name="exp_sum")
        nc.scalar.activation(
            out=exps[:], in_=neg_v[:], func=ACT.Exp, scale=-1.0, bias=neg_max[:], accum_out=exp_sum[:]
        )
        make_residual(end)
        inverse = keep.tile([P, 1], F32, name="inverse")
        nc.vector.reciprocal(out=inverse[:], in_=exp_sum[:])
        soft = keep.tile([P, SPANS], F32, name="soft")
        for e in range(2):
            rows = slice(64 * e, 64 * e + 64)
            nc.vector.tensor_scalar(
                out=soft[rows, :], in0=exps[rows, SPANS * e : SPANS * (e + 1)], scalar1=inverse[rows, :],
                scalar2=None, op0=ALU.mult,
            )

        deltas = {}

        def make_delta(s, kh):
            t = work.tile([P, HALF_C, 4], BF16, name="delta", tag="delta", bufs=3, align_bytes=64)
            src = residual[s][:, :, kh * HALF_C : (kh + 1) * HALF_C].rearrange("p j k -> p k j")
            nc.vector.tensor_scalar(
                out=t[:, :V_COLS, :], in0=src[:, :V_COLS, :], scalar1=soft[:, s : s + 1], scalar2=None, op0=ALU.mult
            )
            nc.scalar.activation(
                out=t[:, V_COLS:, :], in_=src[:, V_COLS:, :], func=ACT.Copy, scale=soft[:, s : s + 1]
            )
            deltas[s, kh] = t

        def quantize_delta(s, kh):
            cols = slice(kh * HALF_C, (kh + 1) * HALF_C)
            nc.vector.quantize_mx(
                out=dl_codes[s][:, cols].bitcast(FP8X4), scales=dl_scales[s][:, cols],
                in_=deltas[s, kh][:].rearrange("p k j -> p (k j)"),
            )

        for kh in range(2):
            make_delta(0, kh)
            for s in range(1, SPANS):
                make_delta(s, kh)
                quantize_delta(s - 1, kh)
            if kh == 0:
                interleave(nc.vector.tensor_copy, SPANS - 1, 0, 64, 64)
                interleave(nc.vector.tensor_copy, SPANS - 1, 1, LAST_SHARE, P - LAST_SHARE)
                quantize_wh(SPANS - 1, 0)
                quantize_wh(SPANS - 1, 1)
            quantize_delta(SPANS - 1, kh)

        def grad_pass(out, s, fg, t, kh):
            feats = slice(fg * STRETCH + t * P, fg * STRETCH + (t + 1) * P)
            cols = slice(kh * HALF_C, (kh + 1) * HALF_C)
            nc.tensor.matmul_mx(
                out=out,
                lhsT=wh_codes[s][:, feats].bitcast(FP8X4),
                lhsT_scale=wh_scales[s][:, feats],
                rhs=dl_codes[s][:, cols].bitcast(FP8X4),
                rhs_scale=dl_scales[s][:, cols],
                start=(s == 0),
                stop=(s == SPANS - 1),
            )

        out_rows = out_0.rearrange("(f p t) k -> f p t k", p=P, t=4)
        out_words = out_1.rearrange("f p m t -> f p (m t)")
        out_sc = keep.tile([P, F_GROUPS, C], U8, name="out_sc", align_bytes=64)

        def finish(fg, kh, banks):
            cols = slice(kh * HALF_C, (kh + 1) * HALF_C)
            res = work.tile([P, 4, HALF_C], F32, name="res", tag="res", bufs=4)
            for t in range(4):
                nc.scalar.activation(
                    out=res[:, t, :], in_=banks[t][:], func=ACT.Copy, scale=out_factor[:, fg, t : t + 1]
                )
            nc.sync.dma_start(out=out_rows[fg][:, :, cols], in_=res[:])
            packed = work.tile([P, HALF_C, 4], BF16, name="packed", tag="packed", bufs=2, align_bytes=64)
            codes = keep.tile([P, HALF_C], U32, name="out_codes_%d_%d" % (fg, kh), align_bytes=64)
            nc.vector.tensor_copy(out=packed[:], in_=res[:].rearrange("p t k -> p k t"))
            nc.vector.quantize_mx(
                out=codes[:].bitcast(FP8X4), scales=out_sc[:, fg, cols], in_=packed[:].rearrange("p k t -> p (k t)")
            )
            nc.sync.dma_start(
                out=out_words[fg][:, 4 * kh * HALF_C : 4 * (kh + 1) * HALF_C].bitcast(I32), in_=codes[:].bitcast(I32)
            )

        grad = [bank(n, [P, HALF_C], "grad_a") for n in range(8)]
        for s in range(SPANS):
            for n in range(8):
                grad_pass(grad[n][:], s, n // 4, n % 4, 0)
        finish(0, 0, grad[:4])
        finish(1, 0, grad[4:])
        grad = [bank(n, [P, HALF_C], "grad_b") for n in range(4)]
        for s in range(SPANS):
            for t in range(4):
                grad_pass(grad[t][:], s, 0, t, 1)
        finish(0, 1, grad)
        grad = [bank(4 + n, [P, HALF_C], "grad_b") for n in range(4)]
        for t in range(4):
            for s in range(SPANS):
                grad_pass(grad[t][:], s, 1, t, 1)
        finish(1, 1, grad)
        for quad in range(4):
            queue = nc.sync if quad % 2 else nc.scalar
            queue.dma_start(
                out=out_2[:, 4 * quad : 4 * quad + 4, :].rearrange("f r m -> r f m").bitcast(I32),
                in_=out_sc[32 * quad : 32 * quad + 4, :, :].bitcast(I32),
            )
